import numpy as np
import ml_dtypes


def mxq(x, axis, fmt="e4m3"):
    dtype, down = {"e4m3": (ml_dtypes.float8_e4m3fn, 7), "e5m2": (ml_dtypes.float8_e5m2, 14)}[fmt]
    v = np.moveaxis(np.asarray(x, np.float32).astype(ml_dtypes.bfloat16).astype(np.float64), axis, -1)
    blocks = v.reshape(v.shape[:-1] + (-1, 32))
    amax = np.abs(blocks).max(-1, keepdims=True)
    byte = np.maximum(np.where(amax > 0, np.frexp(amax)[1] - 1 + 127, 0) - down, 1)
    scale = np.exp2(byte - 127.0)
    codes = (blocks / scale).astype(np.float32).astype(dtype).astype(np.float64)
    return np.moveaxis((codes * scale).reshape(v.shape), -1, axis)


WIDE = False


def mx_kscale(k):
    if not WIDE:
        return np.ones(k)
    levels = np.array([10, -10, 5, -5, 0])
    if k % 512:
        return np.exp2(np.random.permutation(np.resize(levels, k // 32))).repeat(32)
    a = np.empty((k // 512, 16))
    for p in range(k // 512):
        a[p, :8] = np.random.permutation(np.resize(levels, 8))
        for g in range(8):
            far = levels[np.abs(levels - a[p, g]) >= 10]
            a[p, g + 8] = far[np.random.randint(len(far))]
    return np.exp2(a.ravel()).repeat(32)


def f64(x):
    return np.asarray(x).astype(np.float64)


def striped(idx):
    return np.tile(idx.reshape(-1, 16).T, (8, 1)).astype(np.uint16)


def unstriped(offs):
    return offs[:16].T.reshape(-1).astype(np.int64)


def striped8(idx):
    return np.concatenate([x.reshape(-1, 16).T for x in idx]).astype(np.uint16)


def runs(offs, k):
    lists = np.stack([offs[16 * r : 16 * r + 16].T.reshape(-1) for r in range(8)]).astype(np.int64)
    return lists[np.arange(k) % 512 // 64]


def pack_weight(w):
    k, n = w.shape
    w = f64(np.asarray(w, np.float32).astype(ml_dtypes.bfloat16)).reshape(k // 32, 32, n)
    amax = np.abs(w).max(1)
    byte = np.clip(np.where(amax > 0, np.frexp(amax)[1] - 1 + 127 - 7, 1), 1, 254)
    scaled = (w * np.exp2(127.0 - byte)[:, None, :]).reshape(k, n).astype(np.float32)
    words = np.ascontiguousarray(scaled.reshape(k // 512, 128, 4, n).transpose(0, 1, 3, 2)).astype(ml_dtypes.float8_e4m3fn).view(np.uint8)
    return words, np.ascontiguousarray(byte.astype(np.uint8).reshape(k // 512, 16, n))


def unpack_weight(words, scales):
    g, p, n, _ = words.shape
    vals = np.ascontiguousarray(words).view(ml_dtypes.float8_e4m3fn).astype(np.float64) * np.repeat(np.exp2(scales.astype(np.float64) - 127.0), 8, axis=1)[..., None]
    return vals.transpose(0, 1, 3, 2).reshape(g * 512, n)


E2M1 = np.array([0.0, 0.5, 1.0, 1.5, 2.0, 3.0, 4.0, 6.0, -0.0, -0.5, -1.0, -1.5, -2.0, -3.0, -4.0, -6.0])


def pack_fp4(w):
    k, n = w.shape
    w = f64(np.asarray(w, np.float32).astype(ml_dtypes.bfloat16)).reshape(k // 32, 32, n)
    amax = np.abs(w).max(1)
    mant, ex = np.frexp(amax / 6.0)
    byte = np.clip(np.where(amax > 0, np.where(mant > 0.5, ex, ex - 1) + 127, 1), 1, 254)
    scaled = (w * np.exp2(127.0 - byte)[:, None, :]).reshape(k, n).astype(np.float32)
    c = np.ascontiguousarray(scaled.reshape(k // 512, 128, 4, n).transpose(0, 1, 3, 2)).astype(ml_dtypes.float4_e2m1fn).view(np.uint8) & 0xF
    words = (c[..., 0::2] | (c[..., 1::2] << 4)).reshape(k // 512, 128, 2 * n)
    return np.ascontiguousarray(words), np.ascontiguousarray(byte.astype(np.uint8).reshape(k // 512, 16, n))


def unpack_fp4(words, scales):
    g, _, n = scales.shape
    words = np.ascontiguousarray(words).reshape(g, 128, n, 2)
    nib = np.empty((g, 128, n, 4), np.uint8)
    nib[..., 0::2] = words & 0xF
    nib[..., 1::2] = words >> 4
    vals = E2M1[nib] * np.repeat(np.exp2(scales.astype(np.float64) - 127.0), 8, axis=1)[..., None]
    return vals.transpose(0, 1, 3, 2).reshape(g * 512, n)


def planes(y):
    n, m = y.shape
    v = y.astype(np.float32).astype(ml_dtypes.bfloat16).astype(np.float64).reshape(n // 32, 32, m)
    top = np.abs(v).max(1)
    byte = np.clip(np.where(top > 0, np.frexp(top)[1] - 1 + 127 - 7, 1), 1, 254)
    codes = (v * np.exp2(127.0 - byte)[:, None, :]).reshape(n, m).astype(np.float32).astype(ml_dtypes.float8_e4m3fn).view(np.uint8)
    words = codes.reshape(n // 512, 128, 4, m).transpose(0, 1, 3, 2)
    return np.ascontiguousarray(words), np.ascontiguousarray(byte.astype(np.uint8).reshape(n // 512, 16, m))


K, T, S, N, H = 512, 2048, 512, 512, 512


def setup_inputs():
    n = np.random.standard_normal
    s = mx_kscale(K)[:, None]
    u = mx_kscale(H)
    packed_xT = pack_weight(n((K, T)) * s)
    packed_w1 = pack_fp4(n((K, H)) / np.sqrt(K) / s)
    packed_w2 = pack_fp4(n((K, H)) / np.sqrt(K) / s)
    packed_w3 = pack_fp4(n((K, H)) / np.sqrt(K) / s)
    packed_w4 = pack_fp4(n((H, N)) / np.sqrt(H) / u[:, None])
    return {
        "x_words": packed_xT[0],
        "x_scales": packed_xT[1],
        "w1_words": packed_w1[0],
        "w1_scales": packed_w1[1],
        "w2_words": packed_w2[0],
        "w2_scales": packed_w2[1],
        "w3_words": packed_w3[0],
        "w3_scales": packed_w3[1],
        "gn": (np.random.uniform(0.5, 1.5, (H, 1)) * u[:, None]).astype(np.float32),
        "w4_words": packed_w4[0],
        "w4_scales": packed_w4[1],
        "offs": striped(np.random.permutation(T)[:S]),
        "two": striped(np.random.permutation(T)[:S]),
        "three": striped(np.random.permutation(T)[:S]),
        "n1": striped8(np.stack([np.random.permutation(S) for _ in range(8)])),
        "n2": striped8(np.stack([np.random.permutation(S) for _ in range(8)])),
        "n3": striped8(np.stack([np.random.permutation(S) for _ in range(8)])),
        "n4": striped8(np.stack([np.random.permutation(S) for _ in range(8)])),
        "n5": striped8(np.stack([np.random.permutation(S) for _ in range(8)])),
        "n6": striped8(np.stack([np.random.permutation(S) for _ in range(8)])),
    }


def reference(x_words, x_scales, w1_words, w1_scales, w2_words, w2_scales, w3_words, w3_scales, gn, w4_words, w4_scales, offs, two, three, n1, n2, n3, n4, n5, n6):
    xq = unpack_weight(x_words, x_scales)[:, unstriped(offs)]
    y = unpack_fp4(w1_words, w1_scales).T @ xq
    x_two = unpack_weight(x_words, x_scales)[:, unstriped(two)]
    d = unpack_fp4(w2_words, w2_scales).T @ x_two
    m1 = y[np.arange(H)[:, None], runs(n1, H)] - (np.tanh(d) * (d[np.arange(H)[:, None], runs(n2, H)]))
    x_three = unpack_weight(x_words, x_scales)[:, unstriped(three)]
    b = unpack_fp4(w3_words, w3_scales).T @ x_three
    z = f64(gn) * (np.maximum(m1, b[np.arange(H)[:, None], runs(n4, H)]) - (np.minimum(m1[np.arange(H)[:, None], runs(n3, H)], b)))
    h = unpack_fp4(w4_words, w4_scales).T @ mxq(z, 0, "e4m3")
    st = h + h[np.arange(N)[:, None], runs(n5, N)]
    out_0 = st * (np.tanh(st[np.arange(N)[:, None], runs(n6, N)]))
    return (out_0,) + planes(out_0)

@@ -1,0 +1,262 @@
+from contextlib import ExitStack
+
+import concourse.mybir as mybir
+
+F32 = mybir.dt.float32
+BF16 = mybir.dt.bfloat16
+I32 = mybir.dt.int32
+U32 = mybir.dt.uint32
+U16 = mybir.dt.uint16
+U8 = mybir.dt.uint8
+FP8X4 = mybir.dt.float8_e4m3fn_x4
+FP4X4 = mybir.dt.float4_e2m1fn_x4
+ALU = mybir.AluOpType
+ACT = mybir.ActivationFunctionType
+
+P = 128
+PACK = 4
+T = 2048
+S = 512
+FLOPS = 4 * 2 * 512 * 512 * 512
+
+HALVES = [(0, 256), (256, 512)]
+Z_CHUNKS = [(0, 256), (256, 384), (384, 512)]
+
+
+def tile_picked_triosoftbmaxbhopp_none_po_kernel(
+    tc, x_words, x_scales, w1_words, w1_scales, w2_words, w2_scales, w3_words, w3_scales, gn, w4_words, w4_scales,
+    offs, two, three, n1, n2, n3, n4, n5, n6, out_0, out_1, out_2,
+):
+    nc = tc.nc
+    with ExitStack() as ctx:
+        keep = ctx.enter_context(tc.tile_pool(name="keep", bufs=1))
+        ring = ctx.enter_context(tc.tile_pool(name="ring", bufs=3))
+        psum = ctx.enter_context(tc.psum_pool(name="psum", bufs=1))
+
+        def load_list(name, src):
+            tile = keep.tile([P, S // 16], U16, name=name)
+            nc.sync.dma_start(tile[:], src)
+            return tile
+
+        def load_scales(name, src, width):
+            tile = keep.tile([P, width], U8, name=name, align_bytes=64)
+            for q in range(4):
+                rows = src[0][4 * q : 4 * q + 4, :].bitcast(I32)
+                nc.sync.dma_start(tile[32 * q : 32 * q + 32, :].bitcast(I32), rows.unsqueeze(0).to_broadcast([8, 4, width // 4]))
+            return tile
+
+        def load_words(name, src):
+            tile = keep.tile([P, 2 * S], U8, name=name, align_bytes=64)
+            nc.sync.dma_start(tile[:].bitcast(I32), src[0].bitcast(I32))
+            return tile
+
+        def entries(lst, lo, hi):
+            return lst[:, lo // 16 : hi // 16]
+
+        warm = keep.tile([P, 2], F32, name="warm")
+        nc.gpsimd.memset(warm[:], 0.0)
+        nc.scalar.activation(warm[:, 1:2], warm[:, 0:1], ACT.Sigmoid)
+
+        l_two = load_list("l_two", two)
+        xs = load_scales("xs", x_scales, T)
+        l_offs = load_list("l_offs", offs)
+        l_three = load_list("l_three", three)
+        xw = keep.tile([P, T], U32, name="xw", align_bytes=64)
+        nc.sync.dma_start(xw[:].bitcast(I32), x_words[0].rearrange("p c r -> p (c r)").bitcast(I32))
+        w2w = load_words("w2w", w2_words)
+        w2s = load_scales("w2s", w2_scales, S)
+        w1w = load_words("w1w", w1_words)
+        l_n2 = load_list("l_n2", n2)
+        w1s = load_scales("w1s", w1_scales, S)
+        l_n1 = load_list("l_n1", n1)
+        w3w = load_words("w3w", w3_words)
+        w3s = load_scales("w3s", w3_scales, S)
+        l_n4 = load_list("l_n4", n4)
+        l_n3 = load_list("l_n3", n3)
+        gain = keep.tile([P, PACK], F32, name="gain")
+        nc.sync.dma_start(gain[:], gn.rearrange("(p t) o -> p (t o)", t=PACK))
+        w4w = load_words("w4w", w4_words)
+        w4s = load_scales("w4s", w4_scales, S)
+        l_n5 = load_list("l_n5", n5)
+        l_n6 = load_list("l_n6", n6)
+
+        def deal(name, words, scales):
+            dw = keep.tile([P, 2 * S], U8, name=name + "_dw", align_bytes=64)
+            ds = keep.tile([P, S], U8, name=name + "_ds", align_bytes=64)
+            nc.vector.tensor_copy(
+                dw[:].rearrange("p (t m b) -> p t m b", t=PACK, b=2), words[:].rearrange("p (m t b) -> p t m b", t=PACK, b=2)
+            )
+            nc.vector.tensor_copy(ds[:].rearrange("p (t m) -> p t m", t=PACK), scales[:].rearrange("p (m t) -> p t m", t=PACK))
+            return dw, ds
+
+        def pick_scales(name, lst):
+            tile = keep.tile([P, S], U8, name=name, align_bytes=64)
+            nc.vector.tensor_copy(tile[:], xs[:].indirect(lst[:]))
+            return tile
+
+        def pick_words(name, lst):
+            tile = keep.tile([P, S], U32, name=name, align_bytes=64)
+            nc.vector.tensor_copy(tile[:], xw[:].indirect(lst[:]))
+            return tile
+
+        def product(out, weights, t, codes, scales):
+            dw, ds = weights
+            nc.tensor.matmul_mx(
+                out=out,
+                lhsT=dw[:, 2 * P * t : 2 * P * (t + 1)].bitcast(FP4X4),
+                lhsT_scale=ds[:, P * t : P * (t + 1)],
+                rhs=codes.bitcast(FP8X4),
+                rhs_scale=scales,
+                start=True,
+                stop=True,
+            )
+
+        def planes(name):
+            return [keep.tile([P, S], F32, name=f"{name}{t}") for t in range(PACK)]
+
+        def bank(b):
+            return psum.tile([P, S], F32, name=f"bank{b}")
+
+        s_two = pick_scales("s_two", l_two)
+        s_offs = pick_scales("s_offs", l_offs)
+        c_two = pick_words("c_two", l_two)
+        w2 = deal("w2", w2w, w2s)
+        c_offs = pick_words("c_offs", l_offs)
+        w1 = deal("w1", w1w, w1s)
+        s_three = pick_scales("s_three", l_three)
+        c_three = pick_words("c_three", l_three)
+        w3 = deal("w3", w3w, w3s)
+
+        d, tanh_d, y, b, m1 = planes("d"), planes("tanh_d"), planes("y"), planes("b"), planes("m1")
+        d_banks = [bank(t) for t in range(PACK)]
+        y_banks = [bank(PACK + t) for t in range(PACK)]
+        for t in range(PACK):
+            product(d_banks[t][:], w2, t, c_two[:], s_two[:])
+        for t in range(PACK):
+            product(y_banks[t][:], w1, t, c_offs[:], s_offs[:])
+        for t in range(PACK):
+            nc.scalar.copy(d[t][:], d_banks[t][:])
+            nc.scalar.activation(tanh_d[t][:], d_banks[t][:], ACT.Tanh)
+            nc.scalar.copy(y[t][:], y_banks[t][:])
+        for t in range(PACK):
+            b_bank = bank(t)
+            product(b_bank[:], w3, t, c_three[:], s_three[:])
+            nc.scalar.copy(b[t][:], b_bank[:])
+
+        for t in range(PACK):
+            gated = ring.tile([P, S], F32, name="gated")
+            for lo, hi in HALVES:
+                nc.vector.tensor_tensor(gated[:, lo:hi], d[t][:].indirect(entries(l_n2, lo, hi)), tanh_d[t][:, lo:hi], ALU.mult)
+            for lo, hi in HALVES:
+                nc.vector.tensor_tensor(m1[t][:, lo:hi], y[t][:].indirect(entries(l_n1, lo, hi)), gated[:, lo:hi], ALU.subtract)
+
+        h_banks = [bank(PACK + t) for t in range(PACK)]
+        h_window, h_plain = planes("h_window"), planes("h_plain")
+        z_planes = [keep.tile([P, PACK, hi - lo], BF16, name=f"z_planes{c}") for c, (lo, hi) in enumerate(Z_CHUNKS)]
+        units = [(c, t) for c in range(len(Z_CHUNKS)) for t in range(PACK)]
+        state = {}
+        w4 = []
+
+        def fetch_b(c, t):
+            lo, hi = Z_CHUNKS[c]
+            bg = ring.tile([P, hi - lo], F32, name="bg")
+            nc.vector.tensor_copy(bg[:], b[t][:].indirect(entries(l_n4, lo, hi)))
+            state[c, t, "bg"] = bg
+
+        def fetch_m(c, t):
+            lo, hi = Z_CHUNKS[c]
+            mg = ring.tile([P, hi - lo], F32, name="mg")
+            nc.vector.tensor_copy(mg[:], m1[t][:].indirect(entries(l_n3, lo, hi)))
+            state[c, t, "mg"] = mg
+
+        def upper(c, t):
+            lo, hi = Z_CHUNKS[c]
+            up = ring.tile([P, hi - lo], F32, name="up")
+            nc.vector.tensor_tensor(up[:], state[c, t, "bg"][:], m1[t][:, lo:hi], ALU.max)
+            state[c, t, "up"] = up
+
+        def lower(c, t):
+            lo, hi = Z_CHUNKS[c]
+            low = ring.tile([P, hi - lo], F32, name="low")
+            nc.vector.tensor_tensor(low[:], state[c, t, "mg"][:], b[t][:, lo:hi], ALU.min)
+            state[c, t, "low"] = low
+
+        def spread(c, t):
+            lo, hi = Z_CHUNKS[c]
+            gap = ring.tile([P, hi - lo], F32, name="gap")
+            nc.vector.tensor_tensor(gap[:], state[c, t, "up"][:], state[c, t, "low"][:], ALU.subtract)
+            nc.scalar.activation(z_planes[c][:, t, :], gap[:], ACT.Copy, scale=gain[:, t : t + 1])
+
+        def weave(c):
+            lo, hi = Z_CHUNKS[c]
+            woven = keep.tile([P, hi - lo, PACK], BF16, name=f"z_woven{c}", align_bytes=64)
+            if c == len(Z_CHUNKS) - 1:
+                nc.vector.tensor_copy(woven[:], z_planes[c][:].rearrange("p t j -> p j t"))
+            else:
+                nc.scalar.copy(woven[:], z_planes[c][:].rearrange("p t j -> p j t"))
+            state[c, "woven"] = woven
+
+        def second_layer(c):
+            lo, hi = Z_CHUNKS[c]
+            codes = keep.tile([P, hi - lo], U32, name=f"z_codes{c}", align_bytes=64)
+            scales = keep.tile([P, hi - lo], U8, name=f"z_scales{c}", align_bytes=64)
+            nc.vector.quantize_mx(out=codes[:].bitcast(FP8X4), scales=scales[:], in_=state[c, "woven"][:].rearrange("p j t -> p (j t)"))
+            for t in range(PACK):
+                product(h_banks[t][:, lo:hi], w4[0], t, codes[:], scales[:])
+                nc.scalar.activation(h_window[t][:, lo:hi], h_banks[t][:, lo:hi], ACT.Copy, scale=2.0)
+                nc.scalar.activation(h_plain[t][:, lo:hi], h_banks[t][:, lo:hi], ACT.Copy, scale=2.0)
+
+        n_units = len(units)
+        for i in range(n_units + 2):
+            if i < n_units:
+                fetch_b(*units[i])
+            if 0 <= i - 2 < n_units:
+                spread(*units[i - 2])
+                if units[i - 2][1] == PACK - 1:
+                    weave(units[i - 2][0])
+            if 0 <= i - 1 < n_units:
+                upper(*units[i - 1])
+            if i < n_units:
+                fetch_m(*units[i])
+            if 0 <= i - 1 < n_units:
+                lower(*units[i - 1])
+            if i == 2 * PACK:
+                w4.append(deal("w4", w4w, w4s))
+                second_layer(0)
+            if i == 3 * PACK - 1:
+                second_layer(1)
+        second_layer(2)
+
+        st2, sig = planes("st2"), planes("sig")
+        res = [keep.tile([P, PACK, hi - lo], F32, name=f"res{c}") for c, (lo, hi) in enumerate(HALVES)]
+        rows = out_0.rearrange("(p t) j -> p t j", t=PACK)
+
+        def finish(c, t):
+            lo, hi = HALVES[c]
+            nc.vector.scalar_tensor_tensor(res[c][:, t, :], sig[t][:, lo:hi], -0.5, st2[t][:, lo:hi], ALU.add, ALU.mult)
+            nc.sync.dma_start(rows[:, t, lo:hi], res[c][:, t, :])
+
+        for t in range(PACK):
+            for lo, hi in HALVES:
+                nc.vector.tensor_tensor(st2[t][:, lo:hi], h_window[t][:].indirect(entries(l_n5, lo, hi)), h_plain[t][:, lo:hi], ALU.add)
+            for lo, hi in HALVES:
+                nc.scalar.activation(sig[t][:, lo:hi], st2[t][:].indirect(entries(l_n6, lo, hi)), ACT.Sigmoid)
+            if t == 2:
+                finish(0, 0)
+                finish(1, 0)
+        o_codes = keep.tile([P, S], U32, name="o_codes", align_bytes=64)
+        o_scales = keep.tile([P, S], U8, name="o_scales", align_bytes=64)
+        woven_out = [keep.tile([P, hi - lo, PACK], BF16, name=f"o_woven{c}", align_bytes=64) for c, (lo, hi) in enumerate(HALVES)]
+        for c in range(2):
+            for t in range(1, PACK):
+                finish(c, t)
+        nc.scalar.copy(woven_out[0][:], res[0][:].rearrange("p t j -> p j t"))
+        nc.vector.tensor_copy(woven_out[1][:], res[1][:].rearrange("p t j -> p j t"))
+        words_out = out_1[0].rearrange("p c r -> p (c r)").bitcast(I32)
+        for c in (0, 1):
+            lo, hi = HALVES[c]
+            nc.vector.quantize_mx(out=o_codes[:, lo:hi].bitcast(FP8X4), scales=o_scales[:, lo:hi], in_=woven_out[c][:].rearrange("p j t -> p (j t)"))
+            nc.sync.dma_start(words_out[:, lo:hi], o_codes[:, lo:hi].bitcast(I32))
+        for q in range(4):
+            queue = nc.scalar if q % 2 else nc.sync
+            queue.dma_start(out_2[0][4 * q : 4 * q + 4, :].bitcast(I32), o_scales[32 * q : 32 * q + 4, :].bitcast(I32))

@@ -1,6 +1,7 @@
 from contextlib import ExitStack
 
 import concourse.mybir as mybir
+from concourse.masks import make_identity
 
 F32 = mybir.dt.float32
 BF16 = mybir.dt.bfloat16
@@ -20,7 +21,6 @@ S = 512
 FLOPS = 4 * 2 * 512 * 512 * 512
 
 HALVES = [(0, 256), (256, 512)]
-Z_CHUNKS = [(0, 256), (256, 384), (384, 512)]
 
 
 def tile_picked_triosoftbmaxbhopp_none_po_kernel(
@@ -53,6 +53,8 @@ def tile_picked_triosoftbmaxbhopp_none_po_kernel(
         def entries(lst, lo, hi):
             return lst[:, lo // 16 : hi // 16]
 
+        xw = keep.tile([P, T], U32, name="xw", align_bytes=64)
+        nc.scalar.dma_start(xw[:].bitcast(I32), x_words[0].rearrange("p c r -> p (c r)").bitcast(I32))
         warm = keep.tile([P, 2], F32, name="warm")
         nc.gpsimd.memset(warm[:], 0.0)
         nc.scalar.activation(warm[:, 1:2], warm[:, 0:1], ACT.Sigmoid)
@@ -60,23 +62,21 @@ def tile_picked_triosoftbmaxbhopp_none_po_kernel(
         l_two = load_list("l_two", two)
         xs = load_scales("xs", x_scales, T)
         l_offs = load_list("l_offs", offs)
-        l_three = load_list("l_three", three)
-        xw = keep.tile([P, T], U32, name="xw", align_bytes=64)
-        nc.sync.dma_start(xw[:].bitcast(I32), x_words[0].rearrange("p c r -> p (c r)").bitcast(I32))
         w2w = load_words("w2w", w2_words)
         w2s = load_scales("w2s", w2_scales, S)
+        l_three = load_list("l_three", three)
         w1w = load_words("w1w", w1_words)
-        l_n2 = load_list("l_n2", n2)
         w1s = load_scales("w1s", w1_scales, S)
-        l_n1 = load_list("l_n1", n1)
+        l_n2 = load_list("l_n2", n2)
         w3w = load_words("w3w", w3_words)
         w3s = load_scales("w3s", w3_scales, S)
-        l_n4 = load_list("l_n4", n4)
-        l_n3 = load_list("l_n3", n3)
-        gain = keep.tile([P, PACK], F32, name="gain")
-        nc.sync.dma_start(gain[:], gn.rearrange("(p t) o -> p (t o)", t=PACK))
+        l_n1 = load_list("l_n1", n1)
         w4w = load_words("w4w", w4_words)
         w4s = load_scales("w4s", w4_scales, S)
+        l_n4 = load_list("l_n4", n4)
+        l_n3 = load_list("l_n3", n3)
+        gain = keep.tile([P, S], F32, name="gain")
+        nc.sync.dma_start(gain[:], gn.rearrange("i o -> (i o)").partition_broadcast(P))
         l_n5 = load_list("l_n5", n5)
         l_n6 = load_list("l_n6", n6)
 
@@ -87,6 +87,16 @@ def tile_picked_triosoftbmaxbhopp_none_po_kernel(
                 dw[:].rearrange("p (t m b) -> p t m b", t=PACK, b=2), words[:].rearrange("p (m t b) -> p t m b", t=PACK, b=2)
             )
             nc.vector.tensor_copy(ds[:].rearrange("p (t m) -> p t m", t=PACK), scales[:].rearrange("p (m t) -> p t m", t=PACK))
+            return dw, ds
+
+        def deal_runs(name, words, scales):
+            dw = keep.tile([P, 2 * S], U8, name=name + "_dw", align_bytes=64)
+            ds = keep.tile([P, S], U8, name=name + "_ds", align_bytes=64)
+            for dealt, raw in ((dw, words), (ds, scales)):
+                nc.vector.tensor_copy(
+                    dealt[:].bitcast(I32).rearrange("p (a g w) -> p a g w", a=PACK, g=8),
+                    raw[:].bitcast(I32).rearrange("p (g a w) -> p a g w", a=PACK, g=8),
+                )
             return dw, ds
 
         def pick_scales(name, lst):
@@ -117,115 +127,122 @@ def tile_picked_triosoftbmaxbhopp_none_po_kernel(
         def bank(b):
             return psum.tile([P, S], F32, name=f"bank{b}")
 
+        ident = keep.tile([P, P], F32, name="ident")
+        make_identity(nc, ident[:])
+
         s_two = pick_scales("s_two", l_two)
         s_offs = pick_scales("s_offs", l_offs)
         c_two = pick_words("c_two", l_two)
-        w2 = deal("w2", w2w, w2s)
+        w2 = deal_runs("w2", w2w, w2s)
         c_offs = pick_words("c_offs", l_offs)
-        w1 = deal("w1", w1w, w1s)
+        w1 = deal_runs("w1", w1w, w1s)
         s_three = pick_scales("s_three", l_three)
         c_three = pick_words("c_three", l_three)
-        w3 = deal("w3", w3w, w3s)
+        w3 = deal_runs("w3", w3w, w3s)
 
-        d, tanh_d, y, b, m1 = planes("d"), planes("tanh_d"), planes("y"), planes("b"), planes("m1")
-        d_banks = [bank(t) for t in range(PACK)]
-        y_banks = [bank(PACK + t) for t in range(PACK)]
-        for t in range(PACK):
-            product(d_banks[t][:], w2, t, c_two[:], s_two[:])
-        for t in range(PACK):
-            product(y_banks[t][:], w1, t, c_offs[:], s_offs[:])
-        for t in range(PACK):
-            nc.scalar.copy(d[t][:], d_banks[t][:])
-            nc.scalar.activation(tanh_d[t][:], d_banks[t][:], ACT.Tanh)
-            nc.scalar.copy(y[t][:], y_banks[t][:])
-        for t in range(PACK):
-            b_bank = bank(t)
-            product(b_bank[:], w3, t, c_three[:], s_three[:])
-            nc.scalar.copy(b[t][:], b_bank[:])
+        d, neg_b, m1 = planes("d"), planes("neg_b"), planes("m1")
+        y_tanh = [keep.tile([P, 2 * S], F32, name=f"y_tanh{a}") for a in range(PACK)]
+        for a in range(PACK):
+            d_bank = bank(a)
+            product(d_bank[:], w2, a, c_two[:], s_two[:])
+            nc.scalar.copy(d[a][:], d_bank[:])
+            nc.scalar.activation(y_tanh[a][:, S:], d_bank[:], ACT.Tanh)
+            y_bank = bank(PACK + a)
+            product(y_bank[:], w1, a, c_offs[:], s_offs[:])
+            nc.scalar.copy(y_tanh[a][:, :S], y_bank[:])
+        for a in range(PACK):
+            b_bank = bank(a)
+            product(b_bank[:], w3, a, c_three[:], s_three[:])
+            nc.scalar.activation(neg_b[a][:], b_bank[:], ACT.Copy, scale=-1.0)
 
-        for t in range(PACK):
-            gated = ring.tile([P, S], F32, name="gated")
-            for lo, hi in HALVES:
-                nc.vector.tensor_tensor(gated[:, lo:hi], d[t][:].indirect(entries(l_n2, lo, hi)), tanh_d[t][:, lo:hi], ALU.mult)
-            for lo, hi in HALVES:
-                nc.vector.tensor_tensor(m1[t][:, lo:hi], y[t][:].indirect(entries(l_n1, lo, hi)), gated[:, lo:hi], ALU.subtract)
+        n_blocks = S // P
+        z_banks = [bank(PACK + c) for c in range(n_blocks)]
 
-        h_banks = [bank(PACK + t) for t in range(PACK)]
-        h_window, h_plain = planes("h_window"), planes("h_plain")
-        z_planes = [keep.tile([P, PACK, hi - lo], BF16, name=f"z_planes{c}") for c, (lo, hi) in enumerate(Z_CHUNKS)]
-        units = [(c, t) for c in range(len(Z_CHUNKS)) for t in range(PACK)]
-        state = {}
-        w4 = []
+        def add_turned(c, a, src, start=False, stop=False):
+            nc.tensor.matmul(z_banks[c][:, P * a : P * (a + 1)], src, ident[:], start=start, stop=stop, is_transpose=True)
 
-        def fetch_b(c, t):
-            lo, hi = Z_CHUNKS[c]
-            bg = ring.tile([P, hi - lo], F32, name="bg")
-            nc.vector.tensor_copy(bg[:], b[t][:].indirect(entries(l_n4, lo, hi)))
-            state[c, t, "bg"] = bg
+        gated = planes("gated")
 
-        def fetch_m(c, t):
-            lo, hi = Z_CHUNKS[c]
-            mg = ring.tile([P, hi - lo], F32, name="mg")
-            nc.vector.tensor_copy(mg[:], m1[t][:].indirect(entries(l_n3, lo, hi)))
-            state[c, t, "mg"] = mg
+        def gate(a, lo, hi):
+            nc.vector.tensor_tensor(gated[a][:, lo:hi], d[a][:].indirect(entries(l_n2, lo, hi)), y_tanh[a][:, S + lo : S + hi], ALU.mult)
 
-        def upper(c, t):
-            lo, hi = Z_CHUNKS[c]
-            up = ring.tile([P, hi - lo], F32, name="up")
-            nc.vector.tensor_tensor(up[:], state[c, t, "bg"][:], m1[t][:, lo:hi], ALU.max)
-            state[c, t, "up"] = up
+        def meet(a):
+            nc.vector.tensor_tensor(m1[a][:], y_tanh[a][:].indirect(l_n1[:]), gated[a][:], ALU.subtract)
+            for c in range(n_blocks):
+                add_turned(c, a, neg_b[a][:, P * c : P * (c + 1)], start=(a == 0))
+                add_turned(c, a, m1[a][:, P * c : P * (c + 1)])
 
-        def lower(c, t):
-            lo, hi = Z_CHUNKS[c]
-            low = ring.tile([P, hi - lo], F32, name="low")
-            nc.vector.tensor_tensor(low[:], state[c, t, "mg"][:], b[t][:, lo:hi], ALU.min)
-            state[c, t, "low"] = low
+        for a in range(PACK):
+            gate(a, *HALVES[0])
+            if a > 0:
+                meet(a - 1)
+            gate(a, *HALVES[1])
+        w4 = deal("w4", w4w, w4s)
+        meet(PACK - 1)
 
-        def spread(c, t):
-            lo, hi = Z_CHUNKS[c]
-            gap = ring.tile([P, hi - lo], F32, name="gap")
-            nc.vector.tensor_tensor(gap[:], state[c, t, "up"][:], state[c, t, "low"][:], ALU.subtract)
-            nc.scalar.activation(z_planes[c][:, t, :], gap[:], ACT.Copy, scale=gain[:, t : t + 1])
+        h_pair = [keep.tile([P, 2 * S], F32, name=f"h_pair{t}") for t in range(PACK)]
 
-        def weave(c):
-            lo, hi = Z_CHUNKS[c]
-            woven = keep.tile([P, hi - lo, PACK], BF16, name=f"z_woven{c}", align_bytes=64)
-            if c == len(Z_CHUNKS) - 1:
-                nc.vector.tensor_copy(woven[:], z_planes[c][:].rearrange("p t j -> p j t"))
-            else:
-                nc.scalar.copy(woven[:], z_planes[c][:].rearrange("p t j -> p j t"))
-            state[c, "woven"] = woven
+        def h_plain(t, lo, hi):
+            return h_pair[(t - 1) % PACK][:, S + lo : S + hi]
+
+        woven = {}
+
+        def differences(lo, hi, a):
+            diff = ring.tile([P, 2, hi - lo], F32, name="diff")
+            nc.vector.tensor_tensor(diff[:, 0, :], neg_b[a][:].indirect(entries(l_n4, lo, hi)), m1[a][:, lo:hi], ALU.add)
+            nc.vector.tensor_tensor(diff[:, 1, :], m1[a][:].indirect(entries(l_n3, lo, hi)), neg_b[a][:, lo:hi], ALU.add)
+            excess = ring.tile([P, 2, hi - lo], F32, name="excess")
+            nc.scalar.activation(excess[:], diff[:], ACT.Relu, scale=-1.0)
+            for c in range(lo // P, hi // P):
+                for s in range(2):
+                    add_turned(c, a, excess[:, s, P * c - lo : P * (c + 1) - lo], stop=(a == PACK - 1 and s == 1))
+
+        def turn_back(c):
+            z_rows = ring.tile([P, S], BF16, name="z_rows")
+            nc.vector.tensor_tensor(
+                z_rows[:].rearrange("j (g a i) -> j g a i", g=8, a=PACK),
+                z_banks[c][:].rearrange("j (a g i) -> j g a i", g=8, a=PACK),
+                gain[:].rearrange("j (g a i) -> j g a i", g=8, a=PACK),
+                ALU.mult,
+            )
+            pairs = psum.tile([P, 2, P], F32, name=f"bank{c % 2}")
+            words = z_rows[:].bitcast(F32)
+            for u in range(2):
+                nc.tensor.transpose(pairs[:, u, :], words[:, u : 2 * P : 2], ident[:])
+            woven[c] = keep.tile([P, S], BF16, name=f"z_woven{c}", align_bytes=64)
+            nc.scalar.copy(woven[c][:].bitcast(F32).rearrange("p (j u) -> p j u", u=2), pairs[:].rearrange("p u j -> p j u"))
 
         def second_layer(c):
-            lo, hi = Z_CHUNKS[c]
-            codes = keep.tile([P, hi - lo], U32, name=f"z_codes{c}", align_bytes=64)
-            scales = keep.tile([P, hi - lo], U8, name=f"z_scales{c}", align_bytes=64)
-            nc.vector.quantize_mx(out=codes[:].bitcast(FP8X4), scales=scales[:], in_=state[c, "woven"][:].rearrange("p j t -> p (j t)"))
+            codes = keep.tile([P, P], U32, name=f"z_codes{c}", align_bytes=64)
+            scales = keep.tile([P, P], U8, name=f"z_scales{c}", align_bytes=64)
+            nc.vector.quantize_mx(out=codes[:].bitcast(FP8X4), scales=scales[:], in_=woven[c][:])
+            h_bank = psum.tile([P, PACK, P], F32, name=f"bank{2 + c % 2}")
             for t in range(PACK):
-                product(h_banks[t][:, lo:hi], w4[0], t, codes[:], scales[:])
-                nc.scalar.activation(h_window[t][:, lo:hi], h_banks[t][:, lo:hi], ACT.Copy, scale=2.0)
-                nc.scalar.activation(h_plain[t][:, lo:hi], h_banks[t][:, lo:hi], ACT.Copy, scale=2.0)
+                product(h_bank[:, t, :], w4, t, codes[:], scales[:])
+            lo, hi = P * c, P * (c + 1)
+            nc.scalar.activation(h_plain(0, lo, hi), h_bank[:, 0, :], ACT.Copy, scale=2.0)
+            for t in range(PACK):
+                nc.scalar.activation(h_pair[t][:, lo:hi], h_bank[:, t, :], ACT.Copy, scale=2.0)
+                if t + 1 < PACK:
+                    nc.scalar.activation(h_plain(t + 1, lo, hi), h_bank[:, t + 1, :], ACT.Copy, scale=2.0)
 
-        n_units = len(units)
-        for i in range(n_units + 2):
-            if i < n_units:
-                fetch_b(*units[i])
-            if 0 <= i - 2 < n_units:
-                spread(*units[i - 2])
-                if units[i - 2][1] == PACK - 1:
-                    weave(units[i - 2][0])
-            if 0 <= i - 1 < n_units:
-                upper(*units[i - 1])
-            if i < n_units:
-                fetch_m(*units[i])
-            if 0 <= i - 1 < n_units:
-                lower(*units[i - 1])
-            if i == 2 * PACK:
-                w4.append(deal("w4", w4w, w4s))
+        for a in range(PACK):
+            differences(0, 256, a)
+        for a in range(PACK):
+            differences(256, 384, a)
+            if a in (1, 2):
+                turn_back(a - 1)
+        for a in range(PACK):
+            differences(384, 512, a)
+            if a == 0:
                 second_layer(0)
-            if i == 3 * PACK - 1:
+            if a == 1:
                 second_layer(1)
+            if a == 2:
+                turn_back(2)
         second_layer(2)
+        turn_back(3)
+        second_layer(3)
 
         st2, sig = planes("st2"), planes("sig")
         res = [keep.tile([P, PACK, hi - lo], F32, name=f"res{c}") for c, (lo, hi) in enumerate(HALVES)]
@@ -237,8 +254,7 @@ def tile_picked_triosoftbmaxbhopp_none_po_kernel(
             nc.sync.dma_start(rows[:, t, lo:hi], res[c][:, t, :])
 
         for t in range(PACK):
-            for lo, hi in HALVES:
-                nc.vector.tensor_tensor(st2[t][:, lo:hi], h_window[t][:].indirect(entries(l_n5, lo, hi)), h_plain[t][:, lo:hi], ALU.add)
+            nc.vector.tensor_tensor(st2[t][:], h_pair[t][:].indirect(l_n5[:]), h_plain(t, 0, S), ALU.add)
             for lo, hi in HALVES:
                 nc.scalar.activation(sig[t][:, lo:hi], st2[t][:].indirect(entries(l_n6, lo, hi)), ACT.Sigmoid)
             if t == 2:

@@ -31,6 +31,7 @@ def tile_picked_triosoftbmaxbhopp_none_po_kernel(
     with ExitStack() as ctx:
         keep = ctx.enter_context(tc.tile_pool(name="keep", bufs=1))
         ring = ctx.enter_context(tc.tile_pool(name="ring", bufs=3))
+        deep = ctx.enter_context(tc.tile_pool(name="deep", bufs=3))
         psum = ctx.enter_context(tc.psum_pool(name="psum", bufs=1))
 
         def load_list(name, src):
@@ -39,35 +40,38 @@ def tile_picked_triosoftbmaxbhopp_none_po_kernel(
             return tile
 
         def load_scales(name, src, width):
-            tile = keep.tile([P, width], U8, name=name, align_bytes=64)
+            tile = keep.tile([P, width], U8, name=name, tag=name, align_bytes=64)
             for q in range(4):
                 rows = src[0][4 * q : 4 * q + 4, :].bitcast(I32)
                 nc.sync.dma_start(tile[32 * q : 32 * q + 32, :].bitcast(I32), rows.unsqueeze(0).to_broadcast([8, 4, width // 4]))
             return tile
 
         def load_words(name, src):
-            tile = keep.tile([P, 2 * S], U8, name=name, align_bytes=64)
+            tile = keep.tile([P, 2 * S], U8, name=name, tag=name, align_bytes=64)
             nc.sync.dma_start(tile[:].bitcast(I32), src[0].bitcast(I32))
             return tile
 
         def entries(lst, lo, hi):
             return lst[:, lo // 16 : hi // 16]
 
-        xw = keep.tile([P, T], U32, name="xw", align_bytes=64)
-        nc.scalar.dma_start(xw[:].bitcast(I32), x_words[0].rearrange("p c r -> p (c r)").bitcast(I32))
         warm = keep.tile([P, 2], F32, name="warm")
         nc.gpsimd.memset(warm[:], 0.0)
         nc.scalar.activation(warm[:, 1:2], warm[:, 0:1], ACT.Sigmoid)
 
         l_two = load_list("l_two", two)
         xs = load_scales("xs", x_scales, T)
+        l_three = load_list("l_three", three)
         l_offs = load_list("l_offs", offs)
+        xw = keep.tile([P, T], U32, name="xw", align_bytes=64)
+        nc.sync.dma_start(xw[:].bitcast(I32), x_words[0].rearrange("p c r -> p (c r)").bitcast(I32))
         w2w = load_words("w2w", w2_words)
         w2s = load_scales("w2s", w2_scales, S)
-        l_three = load_list("l_three", three)
         w1w = load_words("w1w", w1_words)
         w1s = load_scales("w1s", w1_scales, S)
         l_n2 = load_list("l_n2", n2)
+        d_wide = [keep.tile([P, 2 * S], F32, name=f"d_wide{a}") for a in range(PACK)]
+        gain = d_wide[0][:, S:]
+        nc.sync.dma_start(gain, gn.rearrange("i o -> (i o)").partition_broadcast(P))
         w3w = load_words("w3w", w3_words)
         w3s = load_scales("w3s", w3_scales, S)
         l_n1 = load_list("l_n1", n1)
@@ -75,8 +79,6 @@ def tile_picked_triosoftbmaxbhopp_none_po_kernel(
         w4s = load_scales("w4s", w4_scales, S)
         l_n4 = load_list("l_n4", n4)
         l_n3 = load_list("l_n3", n3)
-        gain = keep.tile([P, S], F32, name="gain")
-        nc.sync.dma_start(gain[:], gn.rearrange("i o -> (i o)").partition_broadcast(P))
         l_n5 = load_list("l_n5", n5)
         l_n6 = load_list("l_n6", n6)
 
@@ -99,13 +101,13 @@ def tile_picked_triosoftbmaxbhopp_none_po_kernel(
                 )
             return dw, ds
 
-        def pick_scales(name, lst):
-            tile = keep.tile([P, S], U8, name=name, align_bytes=64)
+        def pick_scales(name, lst, tag):
+            tile = keep.tile([P, S], U8, name=name, tag=tag, align_bytes=64)
             nc.vector.tensor_copy(tile[:], xs[:].indirect(lst[:]))
             return tile
 
-        def pick_words(name, lst):
-            tile = keep.tile([P, S], U32, name=name, align_bytes=64)
+        def pick_words(name, lst, tag):
+            tile = keep.tile([P, S], U32, name=name, tag=tag, align_bytes=64)
             nc.vector.tensor_copy(tile[:], xw[:].indirect(lst[:]))
             return tile
 
@@ -130,22 +132,22 @@ def tile_picked_triosoftbmaxbhopp_none_po_kernel(
         ident = keep.tile([P, P], F32, name="ident")
         make_identity(nc, ident[:])
 
-        s_two = pick_scales("s_two", l_two)
-        s_offs = pick_scales("s_offs", l_offs)
-        c_two = pick_words("c_two", l_two)
+        s_two = pick_scales("s_two", l_two, "s_two")
+        s_three = pick_scales("s_three", l_three, "s_three")
+        c_two = pick_words("c_two", l_two, "c_two")
         w2 = deal_runs("w2", w2w, w2s)
-        c_offs = pick_words("c_offs", l_offs)
+        s_offs = pick_scales("s_offs", l_offs, "w2s")
+        c_offs = pick_words("c_offs", l_offs, "w2w")
         w1 = deal_runs("w1", w1w, w1s)
-        s_three = pick_scales("s_three", l_three)
-        c_three = pick_words("c_three", l_three)
+        c_three = pick_words("c_three", l_three, "c_three")
         w3 = deal_runs("w3", w3w, w3s)
 
-        d, neg_b, m1 = planes("d"), planes("neg_b"), planes("m1")
+        neg_b, m1 = planes("neg_b"), planes("m1")
         y_tanh = [keep.tile([P, 2 * S], F32, name=f"y_tanh{a}") for a in range(PACK)]
         for a in range(PACK):
             d_bank = bank(a)
             product(d_bank[:], w2, a, c_two[:], s_two[:])
-            nc.scalar.copy(d[a][:], d_bank[:])
+            nc.scalar.copy(d_wide[a][:, :S], d_bank[:])
             nc.scalar.activation(y_tanh[a][:, S:], d_bank[:], ACT.Tanh)
             y_bank = bank(PACK + a)
             product(y_bank[:], w1, a, c_offs[:], s_offs[:])
@@ -159,90 +161,99 @@ def tile_picked_triosoftbmaxbhopp_none_po_kernel(
         z_banks = [bank(PACK + c) for c in range(n_blocks)]
 
         def add_turned(c, a, src, start=False, stop=False):
-            nc.tensor.matmul(z_banks[c][:, P * a : P * (a + 1)], src, ident[:], start=start, stop=stop, is_transpose=True)
+            nc.tensor.matmul(z_banks[c][:].rearrange("j (g a i) -> j g a i", g=8, a=PACK)[:, :, a, :], src, ident[:], start=start, stop=stop, is_transpose=True)
 
-        gated = planes("gated")
+        gated_last = keep.tile([P, S], F32, name="gated_last")
+        gated = [d_wide[a + 1][:, S:] for a in range(PACK - 1)] + [gated_last[:]]
 
-        def gate(a, lo, hi):
-            nc.vector.tensor_tensor(gated[a][:, lo:hi], d[a][:].indirect(entries(l_n2, lo, hi)), y_tanh[a][:, S + lo : S + hi], ALU.mult)
+        def gate(a):
+            nc.vector.tensor_tensor(gated[a], d_wide[a][:].indirect(l_n2[:]), y_tanh[a][:, S:], ALU.mult)
 
         def meet(a):
-            nc.vector.tensor_tensor(m1[a][:], y_tanh[a][:].indirect(l_n1[:]), gated[a][:], ALU.subtract)
+            nc.vector.tensor_tensor(m1[a][:], y_tanh[a][:].indirect(l_n1[:]), gated[a], ALU.subtract)
             for c in range(n_blocks):
                 add_turned(c, a, neg_b[a][:, P * c : P * (c + 1)], start=(a == 0))
                 add_turned(c, a, m1[a][:, P * c : P * (c + 1)])
 
-        for a in range(PACK):
-            gate(a, *HALVES[0])
-            if a > 0:
-                meet(a - 1)
-            gate(a, *HALVES[1])
+        gate(0)
         w4 = deal("w4", w4w, w4s)
-        meet(PACK - 1)
+        for a in range(1, PACK):
+            gate(a)
+            meet(a - 1)
 
-        h_pair = [keep.tile([P, 2 * S], F32, name=f"h_pair{t}") for t in range(PACK)]
-
-        def h_plain(t, lo, hi):
-            return h_pair[(t - 1) % PACK][:, S + lo : S + hi]
-
+        h_plain = keep.tile([P, PACK, S], F32, name="h_plain")
         woven = {}
 
-        def differences(lo, hi, a):
-            diff = ring.tile([P, 2, hi - lo], F32, name="diff")
+        def differences(c, a):
+            lo, hi = P * c, P * (c + 1)
+            diff = deep.tile([P, 2, P], F32, name="diff")
             nc.vector.tensor_tensor(diff[:, 0, :], neg_b[a][:].indirect(entries(l_n4, lo, hi)), m1[a][:, lo:hi], ALU.add)
             nc.vector.tensor_tensor(diff[:, 1, :], m1[a][:].indirect(entries(l_n3, lo, hi)), neg_b[a][:, lo:hi], ALU.add)
-            excess = ring.tile([P, 2, hi - lo], F32, name="excess")
-            nc.scalar.activation(excess[:], diff[:], ACT.Relu, scale=-1.0)
-            for c in range(lo // P, hi // P):
+            excess = deep.tile([P, 2, P], F32, name="excess")
+            if (c, a) == (n_blocks - 1, PACK - 1):
                 for s in range(2):
-                    add_turned(c, a, excess[:, s, P * c - lo : P * (c + 1) - lo], stop=(a == PACK - 1 and s == 1))
+                    nc.vector.tensor_scalar(excess[:, s, :], diff[:, s, :], 0.0, -1.0, ALU.min, ALU.mult)
+            else:
+                nc.scalar.activation(excess[:], diff[:], ACT.Relu, scale=-1.0)
+            for s in range(2):
+                add_turned(c, a, excess[:, s, :], stop=(a == PACK - 1 and s == 1))
 
         def turn_back(c):
-            z_rows = ring.tile([P, S], BF16, name="z_rows")
-            nc.vector.tensor_tensor(
-                z_rows[:].rearrange("j (g a i) -> j g a i", g=8, a=PACK),
-                z_banks[c][:].rearrange("j (a g i) -> j g a i", g=8, a=PACK),
-                gain[:].rearrange("j (g a i) -> j g a i", g=8, a=PACK),
-                ALU.mult,
-            )
+            last = c == n_blocks - 1
+            if c == n_blocks - 2:
+                z_rows = m1[PACK - 1][:, : S // 2].bitcast(BF16).rearrange("j (u p e) -> j u p e", u=2, e=2)
+            else:
+                z_rows = ring.tile([P, 2, P, 2], BF16, name="z_rows")
             pairs = psum.tile([P, 2, P], F32, name=f"bank{c % 2}")
-            words = z_rows[:].bitcast(F32)
-            for u in range(2):
-                nc.tensor.transpose(pairs[:, u, :], words[:, u : 2 * P : 2], ident[:])
+            sums = z_banks[c][:].rearrange("j (p u e) -> j u p e", u=2, e=2)
+            gains = gain.rearrange("j (p u e) -> j u p e", u=2, e=2)
+            for us in ([slice(0, 1), slice(1, 2)] if last else [slice(0, 2)]):
+                nc.vector.tensor_tensor(z_rows[:, us], sums[:, us], gains[:, us], ALU.mult)
+                for u in range(us.start, us.stop):
+                    nc.tensor.transpose(pairs[:, u, :], z_rows[:, u].rearrange("j p e -> j (p e)").bitcast(F32), ident[:])
             woven[c] = keep.tile([P, S], BF16, name=f"z_woven{c}", align_bytes=64)
-            nc.scalar.copy(woven[c][:].bitcast(F32).rearrange("p (j u) -> p j u", u=2), pairs[:].rearrange("p u j -> p j u"))
+            words = woven[c][:].bitcast(F32).rearrange("p (j u) -> p j u", u=2)
+            if last:
+                nc.vector.tensor_copy(words, pairs[:].rearrange("p u j -> p j u"))
+            else:
+                nc.scalar.copy(words, pairs[:].rearrange("p u j -> p j u"))
 
         def second_layer(c):
             codes = keep.tile([P, P], U32, name=f"z_codes{c}", align_bytes=64)
             scales = keep.tile([P, P], U8, name=f"z_scales{c}", align_bytes=64)
             nc.vector.quantize_mx(out=codes[:].bitcast(FP8X4), scales=scales[:], in_=woven[c][:])
-            h_bank = psum.tile([P, PACK, P], F32, name=f"bank{2 + c % 2}")
-            for t in range(PACK):
-                product(h_bank[:, t, :], w4, t, codes[:], scales[:])
             lo, hi = P * c, P * (c + 1)
-            nc.scalar.activation(h_plain(0, lo, hi), h_bank[:, 0, :], ACT.Copy, scale=2.0)
-            for t in range(PACK):
-                nc.scalar.activation(h_pair[t][:, lo:hi], h_bank[:, t, :], ACT.Copy, scale=2.0)
-                if t + 1 < PACK:
-                    nc.scalar.activation(h_plain(t + 1, lo, hi), h_bank[:, t + 1, :], ACT.Copy, scale=2.0)
+            if c < n_blocks - 1:
+                h_bank = psum.tile([P, PACK, P], F32, name=f"bank{2 + c % 2}")
+                for t in range(PACK):
+                    product(h_bank[:, t, :], w4, t, codes[:], scales[:])
+                nc.scalar.activation(y_tanh[0][:, lo:hi], h_bank[:, 0, :], ACT.Copy, scale=2.0)
+                nc.scalar.activation(h_plain[:, :, lo:hi], h_bank[:], ACT.Copy, scale=2.0)
+                for t in range(1, PACK):
+                    nc.scalar.activation(y_tanh[t][:, lo:hi], h_bank[:, t, :], ACT.Copy, scale=2.0)
+            else:
+                h_last = [psum.tile([P, P], F32, name=f"bank{PACK + t}") for t in range(PACK)]
+                for t in range(PACK):
+                    product(h_last[t][:], w4, t, codes[:], scales[:])
+                nc.vector.tensor_scalar(y_tanh[0][:, lo:hi], h_last[0][:], 2.0, None, ALU.mult)
+                nc.vector.tensor_scalar(h_plain[:, 0, lo:hi], h_last[0][:], 2.0, None, ALU.mult)
+                for t in range(1, PACK):
+                    nc.scalar.activation(y_tanh[t][:, lo:hi], h_last[t][:], ACT.Copy, scale=2.0)
+                    nc.scalar.activation(h_plain[:, t, lo:hi], h_last[t][:], ACT.Copy, scale=2.0)
 
-        for a in range(PACK):
-            differences(0, 256, a)
-        for a in range(PACK):
-            differences(256, 384, a)
-            if a in (1, 2):
-                turn_back(a - 1)
-        for a in range(PACK):
-            differences(384, 512, a)
-            if a == 0:
-                second_layer(0)
-            if a == 1:
-                second_layer(1)
-            if a == 2:
-                turn_back(2)
-        second_layer(2)
-        turn_back(3)
-        second_layer(3)
+        for c in range(n_blocks):
+            for a in range(PACK):
+                if (c, a) == (0, 1):
+                    meet(PACK - 1)
+                differences(c, a)
+                if a == 0 and c >= 2:
+                    second_layer(c - 2)
+                if a == 1 and 1 <= c < n_blocks - 1:
+                    turn_back(c - 1)
+        turn_back(n_blocks - 2)
+        turn_back(n_blocks - 1)
+        second_layer(n_blocks - 2)
+        second_layer(n_blocks - 1)
 
         st2, sig = planes("st2"), planes("sig")
         res = [keep.tile([P, PACK, hi - lo], F32, name=f"res{c}") for c, (lo, hi) in enumerate(HALVES)]
@@ -253,23 +264,20 @@ def tile_picked_triosoftbmaxbhopp_none_po_kernel(
             nc.vector.scalar_tensor_tensor(res[c][:, t, :], sig[t][:, lo:hi], -0.5, st2[t][:, lo:hi], ALU.add, ALU.mult)
             nc.sync.dma_start(rows[:, t, lo:hi], res[c][:, t, :])
 
+        early = {1: [(0, 0)], 2: [(1, 0), (0, 1)], 3: [(1, 1), (0, 2), (0, 3), (1, 2), (1, 3)]}
         for t in range(PACK):
-            nc.vector.tensor_tensor(st2[t][:], h_pair[t][:].indirect(l_n5[:]), h_plain(t, 0, S), ALU.add)
+            nc.vector.tensor_tensor(st2[t][:], y_tanh[t][:].indirect(l_n5[:]), h_plain[:, t, :], ALU.add)
             for lo, hi in HALVES:
                 nc.scalar.activation(sig[t][:, lo:hi], st2[t][:].indirect(entries(l_n6, lo, hi)), ACT.Sigmoid)
-            if t == 2:
-                finish(0, 0)
-                finish(1, 0)
+            for c, done in early.get(t, []):
+                finish(c, done)
         o_codes = keep.tile([P, S], U32, name="o_codes", align_bytes=64)
         o_scales = keep.tile([P, S], U8, name="o_scales", align_bytes=64)
         woven_out = [keep.tile([P, hi - lo, PACK], BF16, name=f"o_woven{c}", align_bytes=64) for c, (lo, hi) in enumerate(HALVES)]
-        for c in range(2):
-            for t in range(1, PACK):
-                finish(c, t)
         nc.scalar.copy(woven_out[0][:], res[0][:].rearrange("p t j -> p j t"))
         nc.vector.tensor_copy(woven_out[1][:], res[1][:].rearrange("p t j -> p j t"))
         words_out = out_1[0].rearrange("p c r -> p (c r)").bitcast(I32)
-        for c in (0, 1):
+        for c in (1, 0):
             lo, hi = HALVES[c]
             nc.vector.quantize_mx(out=o_codes[:, lo:hi].bitcast(FP8X4), scales=o_scales[:, lo:hi], in_=woven_out[c][:].rearrange("p j t -> p (j t)"))
             nc.sync.dma_start(words_out[:, lo:hi], o_codes[:, lo:hi].bitcast(I32))

@@ -62,16 +62,15 @@ def tile_picked_triosoftbmaxbhopp_none_po_kernel(
         xs = load_scales("xs", x_scales, T)
         l_three = load_list("l_three", three)
         l_offs = load_list("l_offs", offs)
-        xw = keep.tile([P, T], U32, name="xw", align_bytes=64)
+        xw = keep.tile([P, T], U32, name="xw", tag="xw", align_bytes=64)
         nc.sync.dma_start(xw[:].bitcast(I32), x_words[0].rearrange("p c r -> p (c r)").bitcast(I32))
         w2w = load_words("w2w", w2_words)
         w2s = load_scales("w2s", w2_scales, S)
+        gain_cols = keep.tile([P, PACK], F32, name="gain_cols")
+        nc.sync.dma_start(gain_cols[:], gn.rearrange("(p t) o -> p (t o)", t=PACK))
         w1w = load_words("w1w", w1_words)
         w1s = load_scales("w1s", w1_scales, S)
         l_n2 = load_list("l_n2", n2)
-        d_wide = [keep.tile([P, 2 * S], F32, name=f"d_wide{a}") for a in range(PACK)]
-        gain = d_wide[0][:, S:]
-        nc.sync.dma_start(gain, gn.rearrange("i o -> (i o)").partition_broadcast(P))
         w3w = load_words("w3w", w3_words)
         w3s = load_scales("w3s", w3_scales, S)
         l_n1 = load_list("l_n1", n1)
@@ -82,18 +81,18 @@ def tile_picked_triosoftbmaxbhopp_none_po_kernel(
         l_n5 = load_list("l_n5", n5)
         l_n6 = load_list("l_n6", n6)
 
-        def deal(name, words, scales):
-            dw = keep.tile([P, 2 * S], U8, name=name + "_dw", align_bytes=64)
-            ds = keep.tile([P, S], U8, name=name + "_ds", align_bytes=64)
+        def deal(name, words, scales, tags):
+            dw = keep.tile([P, 2 * S], U8, name=name + "_dw", tag=tags[0], align_bytes=64)
+            ds = keep.tile([P, S], U8, name=name + "_ds", tag=tags[1], align_bytes=64)
             nc.vector.tensor_copy(
                 dw[:].rearrange("p (t m b) -> p t m b", t=PACK, b=2), words[:].rearrange("p (m t b) -> p t m b", t=PACK, b=2)
             )
             nc.vector.tensor_copy(ds[:].rearrange("p (t m) -> p t m", t=PACK), scales[:].rearrange("p (m t) -> p t m", t=PACK))
             return dw, ds
 
-        def deal_runs(name, words, scales):
-            dw = keep.tile([P, 2 * S], U8, name=name + "_dw", align_bytes=64)
-            ds = keep.tile([P, S], U8, name=name + "_ds", align_bytes=64)
+        def deal_runs(name, words, scales, tags):
+            dw = keep.tile([P, 2 * S], U8, name=name + "_dw", tag=tags[0], align_bytes=64)
+            ds = keep.tile([P, S], U8, name=name + "_ds", tag=tags[1], align_bytes=64)
             for dealt, raw in ((dw, words), (ds, scales)):
                 nc.vector.tensor_copy(
                     dealt[:].bitcast(I32).rearrange("p (a g w) -> p a g w", a=PACK, g=8),
@@ -132,15 +131,22 @@ def tile_picked_triosoftbmaxbhopp_none_po_kernel(
         ident = keep.tile([P, P], F32, name="ident")
         make_identity(nc, ident[:])
 
+        d_wide = [keep.tile([P, 2 * S], F32, name=f"d_wide{a}") for a in range(PACK)]
+        gains = d_wide[0][:, S:].rearrange("j (u p e) -> j u p e", u=2, e=2)
+        gain_bank = psum.tile([P, PACK, P], F32, name=f"bank{PACK}")
+        for t in range(PACK):
+            nc.tensor.transpose(gain_bank[:, t, :], gain_cols[:, t : t + 1].to_broadcast([P, P]), ident[:])
+        nc.scalar.copy(gains, gain_bank[:].rearrange("j (u e) p -> j u p e", u=2))
+
         s_two = pick_scales("s_two", l_two, "s_two")
         s_three = pick_scales("s_three", l_three, "s_three")
         c_two = pick_words("c_two", l_two, "c_two")
-        w2 = deal_runs("w2", w2w, w2s)
+        w2 = deal_runs("w2", w2w, w2s, ("w2_dw", "w2_ds"))
         s_offs = pick_scales("s_offs", l_offs, "w2s")
         c_offs = pick_words("c_offs", l_offs, "w2w")
-        w1 = deal_runs("w1", w1w, w1s)
+        w1 = deal_runs("w1", w1w, w1s, ("xs", "w1w"))
         c_three = pick_words("c_three", l_three, "c_three")
-        w3 = deal_runs("w3", w3w, w3s)
+        w3 = deal_runs("w3", w3w, w3s, ("xw", "w3w"))
 
         neg_b, m1 = planes("neg_b"), planes("m1")
         y_tanh = [keep.tile([P, 2 * S], F32, name=f"y_tanh{a}") for a in range(PACK)]
@@ -176,7 +182,7 @@ def tile_picked_triosoftbmaxbhopp_none_po_kernel(
                 add_turned(c, a, m1[a][:, P * c : P * (c + 1)])
 
         gate(0)
-        w4 = deal("w4", w4w, w4s)
+        w4 = deal("w4", w4w, w4s, ("w3s", "w4w"))
         for a in range(1, PACK):
             gate(a)
             meet(a - 1)
@@ -184,19 +190,20 @@ def tile_picked_triosoftbmaxbhopp_none_po_kernel(
         h_plain = keep.tile([P, PACK, S], F32, name="h_plain")
         woven = {}
 
-        def differences(c, a):
-            lo, hi = P * c, P * (c + 1)
-            diff = deep.tile([P, 2, P], F32, name="diff")
+        def differences(first, count, a):
+            lo, hi = P * first, P * (first + count)
+            diff = deep.tile([P, 2, hi - lo], F32, name="diff")
             nc.vector.tensor_tensor(diff[:, 0, :], neg_b[a][:].indirect(entries(l_n4, lo, hi)), m1[a][:, lo:hi], ALU.add)
             nc.vector.tensor_tensor(diff[:, 1, :], m1[a][:].indirect(entries(l_n3, lo, hi)), neg_b[a][:, lo:hi], ALU.add)
-            excess = deep.tile([P, 2, P], F32, name="excess")
-            if (c, a) == (n_blocks - 1, PACK - 1):
+            excess = deep.tile([P, 2, hi - lo], F32, name="excess")
+            if (first, a) == (n_blocks - 1, PACK - 1):
                 for s in range(2):
                     nc.vector.tensor_scalar(excess[:, s, :], diff[:, s, :], 0.0, -1.0, ALU.min, ALU.mult)
             else:
                 nc.scalar.activation(excess[:], diff[:], ACT.Relu, scale=-1.0)
-            for s in range(2):
-                add_turned(c, a, excess[:, s, :], stop=(a == PACK - 1 and s == 1))
+            for c in range(count):
+                for s in range(2):
+                    add_turned(first + c, a, excess[:, s, P * c : P * (c + 1)], stop=(a == PACK - 1 and s == 1))
 
         def turn_back(c):
             last = c == n_blocks - 1
@@ -206,7 +213,6 @@ def tile_picked_triosoftbmaxbhopp_none_po_kernel(
                 z_rows = ring.tile([P, 2, P, 2], BF16, name="z_rows")
             pairs = psum.tile([P, 2, P], F32, name=f"bank{c % 2}")
             sums = z_banks[c][:].rearrange("j (p u e) -> j u p e", u=2, e=2)
-            gains = gain.rearrange("j (p u e) -> j u p e", u=2, e=2)
             for us in ([slice(0, 1), slice(1, 2)] if last else [slice(0, 2)]):
                 nc.vector.tensor_tensor(z_rows[:, us], sums[:, us], gains[:, us], ALU.mult)
                 for u in range(us.start, us.stop):
@@ -241,41 +247,55 @@ def tile_picked_triosoftbmaxbhopp_none_po_kernel(
                     nc.scalar.activation(y_tanh[t][:, lo:hi], h_last[t][:], ACT.Copy, scale=2.0)
                     nc.scalar.activation(h_plain[:, t, lo:hi], h_last[t][:], ACT.Copy, scale=2.0)
 
-        for c in range(n_blocks):
-            for a in range(PACK):
-                if (c, a) == (0, 1):
-                    meet(PACK - 1)
-                differences(c, a)
-                if a == 0 and c >= 2:
-                    second_layer(c - 2)
-                if a == 1 and 1 <= c < n_blocks - 1:
-                    turn_back(c - 1)
+        for a in range(PACK):
+            if a == 1:
+                meet(PACK - 1)
+            differences(0, 2, a)
+        for a in range(PACK):
+            differences(2, 1, a)
+            if a in (1, 2):
+                turn_back(a - 1)
+        for a in range(PACK):
+            differences(3, 1, a)
+            if a in (0, 1):
+                second_layer(a)
         turn_back(n_blocks - 2)
         turn_back(n_blocks - 1)
         second_layer(n_blocks - 2)
         second_layer(n_blocks - 1)
 
         st2, sig = planes("st2"), planes("sig")
-        res = [keep.tile([P, PACK, hi - lo], F32, name=f"res{c}") for c, (lo, hi) in enumerate(HALVES)]
-        rows = out_0.rearrange("(p t) j -> p t j", t=PACK)
+        half = S // 2
+        res = keep.tile([P, 2, PACK, half], F32, name="res")
+        rows = out_0.rearrange("(p t) (c j) -> p c t j", t=PACK, c=2)
 
-        def finish(c, t):
-            lo, hi = HALVES[c]
-            nc.vector.scalar_tensor_tensor(res[c][:, t, :], sig[t][:, lo:hi], -0.5, st2[t][:, lo:hi], ALU.add, ALU.mult)
-            nc.sync.dma_start(rows[:, t, lo:hi], res[c][:, t, :])
+        def finish(t, cs):
+            cols = slice(half * cs.start, half * cs.stop)
+            nc.vector.scalar_tensor_tensor(
+                res[:, cs, t, :],
+                sig[t][:, cols].rearrange("p (c j) -> p c j", j=half),
+                -0.5,
+                st2[t][:, cols].rearrange("p (c j) -> p c j", j=half),
+                ALU.add,
+                ALU.mult,
+            )
+            nc.sync.dma_start(rows[:, cs, t, :], res[:, cs, t, :])
 
-        early = {1: [(0, 0)], 2: [(1, 0), (0, 1)], 3: [(1, 1), (0, 2), (0, 3), (1, 2), (1, 3)]}
         for t in range(PACK):
             nc.vector.tensor_tensor(st2[t][:], y_tanh[t][:].indirect(l_n5[:]), h_plain[:, t, :], ALU.add)
             for lo, hi in HALVES:
                 nc.scalar.activation(sig[t][:, lo:hi], st2[t][:].indirect(entries(l_n6, lo, hi)), ACT.Sigmoid)
-            for c, done in early.get(t, []):
-                finish(c, done)
+            if t == PACK - 2:
+                finish(0, slice(0, 2))
+                finish(1, slice(0, 2))
+        finish(2, slice(0, 2))
+        finish(3, slice(0, 1))
+        finish(3, slice(1, 2))
         o_codes = keep.tile([P, S], U32, name="o_codes", align_bytes=64)
         o_scales = keep.tile([P, S], U8, name="o_scales", align_bytes=64)
         woven_out = [keep.tile([P, hi - lo, PACK], BF16, name=f"o_woven{c}", align_bytes=64) for c, (lo, hi) in enumerate(HALVES)]
-        nc.scalar.copy(woven_out[0][:], res[0][:].rearrange("p t j -> p j t"))
-        nc.vector.tensor_copy(woven_out[1][:], res[1][:].rearrange("p t j -> p j t"))
+        nc.scalar.copy(woven_out[0][:], res[:, 0].rearrange("p t j -> p j t"))
+        nc.vector.tensor_copy(woven_out[1][:], res[:, 1].rearrange("p t j -> p j t"))
         words_out = out_1[0].rearrange("p c r -> p (c r)").bitcast(I32)
         for c in (1, 0):
             lo, hi = HALVES[c]

@@ -16,11 +16,13 @@ ACT = mybir.ActivationFunctionType
 
 P = 128
 PACK = 4
+RUNS = 8
 T = 2048
 S = 512
+BLOCKS = S // P
+HALF = S // 2
+SCALAR_WEAVE = 192
 FLOPS = 4 * 2 * 512 * 512 * 512
-
-HALVES = [(0, 256), (256, 512)]
 
 
 def tile_picked_triosoftbmaxbhopp_none_po_kernel(
@@ -31,143 +33,135 @@ def tile_picked_triosoftbmaxbhopp_none_po_kernel(
     with ExitStack() as ctx:
         keep = ctx.enter_context(tc.tile_pool(name="keep", bufs=1))
         ring = ctx.enter_context(tc.tile_pool(name="ring", bufs=3))
-        deep = ctx.enter_context(tc.tile_pool(name="deep", bufs=3))
         psum = ctx.enter_context(tc.psum_pool(name="psum", bufs=1))
+
+        def bank(b, shape):
+            return psum.tile(shape, F32, name=f"bank{b}")
+
+        def tiles(name, width):
+            return [keep.tile([P, width], F32, name=f"{name}{n}") for n in range(PACK)]
+
+        def entries(offsets, lo, hi):
+            return offsets[:, lo // 16 : hi // 16]
 
         def load_list(name, src):
             tile = keep.tile([P, S // 16], U16, name=name)
             nc.sync.dma_start(tile[:], src)
             return tile
 
-        def load_scales(name, src, width):
+        def load_scales(name, src, width, queues):
             tile = keep.tile([P, width], U8, name=name, tag=name, align_bytes=64)
             for q in range(4):
-                rows = src[0][4 * q : 4 * q + 4, :].bitcast(I32)
-                nc.sync.dma_start(tile[32 * q : 32 * q + 32, :].bitcast(I32), rows.unsqueeze(0).to_broadcast([8, 4, width // 4]))
+                rows = src[0][4 * q : 4 * q + 4, :].bitcast(I32).unsqueeze(0).to_broadcast([8, 4, width // 4])
+                queues[q % len(queues)].dma_start(tile[32 * q : 32 * q + 32, :].bitcast(I32), rows)
             return tile
 
-        def load_words(name, src):
-            tile = keep.tile([P, 2 * S], U8, name=name, tag=name, align_bytes=64)
-            nc.sync.dma_start(tile[:].bitcast(I32), src[0].bitcast(I32))
-            return tile
-
-        def entries(lst, lo, hi):
-            return lst[:, lo // 16 : hi // 16]
-
-        warm = keep.tile([P, 2], F32, name="warm")
-        nc.gpsimd.memset(warm[:], 0.0)
-        nc.scalar.activation(warm[:, 1:2], warm[:, 0:1], ACT.Sigmoid)
+        def load_weight(name, words, scales):
+            tile = keep.tile([P, 2 * S], U8, name=name + "_words", tag=name + "_words", align_bytes=64)
+            nc.sync.dma_start(tile[:].bitcast(I32), words[0].bitcast(I32))
+            return tile, load_scales(name + "_scales", scales, S, [nc.sync])
 
         l_two = load_list("l_two", two)
-        xs = load_scales("xs", x_scales, T)
+        xs = load_scales("xs", x_scales, T, [nc.sync, nc.scalar])
         l_three = load_list("l_three", three)
         l_offs = load_list("l_offs", offs)
         xw = keep.tile([P, T], U32, name="xw", tag="xw", align_bytes=64)
         nc.sync.dma_start(xw[:].bitcast(I32), x_words[0].rearrange("p c r -> p (c r)").bitcast(I32))
-        w2w = load_words("w2w", w2_words)
-        w2s = load_scales("w2s", w2_scales, S)
+        w2_raw = load_weight("w2", w2_words, w2_scales)
         gain_cols = keep.tile([P, PACK], F32, name="gain_cols")
         nc.sync.dma_start(gain_cols[:], gn.rearrange("(p t) o -> p (t o)", t=PACK))
-        w1w = load_words("w1w", w1_words)
-        w1s = load_scales("w1s", w1_scales, S)
+        w1_raw = load_weight("w1", w1_words, w1_scales)
         l_n2 = load_list("l_n2", n2)
-        w3w = load_words("w3w", w3_words)
-        w3s = load_scales("w3s", w3_scales, S)
+        w3_raw = load_weight("w3", w3_words, w3_scales)
         l_n1 = load_list("l_n1", n1)
-        w4w = load_words("w4w", w4_words)
-        w4s = load_scales("w4s", w4_scales, S)
+        w4_raw = load_weight("w4", w4_words, w4_scales)
         l_n4 = load_list("l_n4", n4)
         l_n3 = load_list("l_n3", n3)
         l_n5 = load_list("l_n5", n5)
         l_n6 = load_list("l_n6", n6)
 
-        def deal(name, words, scales, tags):
-            dw = keep.tile([P, 2 * S], U8, name=name + "_dw", tag=tags[0], align_bytes=64)
-            ds = keep.tile([P, S], U8, name=name + "_ds", tag=tags[1], align_bytes=64)
-            nc.vector.tensor_copy(
-                dw[:].rearrange("p (t m b) -> p t m b", t=PACK, b=2), words[:].rearrange("p (m t b) -> p t m b", t=PACK, b=2)
-            )
-            nc.vector.tensor_copy(ds[:].rearrange("p (t m) -> p t m", t=PACK), scales[:].rearrange("p (m t) -> p t m", t=PACK))
-            return dw, ds
+        warm = keep.tile([P, 2], F32, name="warm")
+        nc.gpsimd.memset(warm[:], 0.0)
+        nc.scalar.activation(warm[:, 1:2], warm[:, 0:1], ACT.Sigmoid)
 
-        def deal_runs(name, words, scales, tags):
-            dw = keep.tile([P, 2 * S], U8, name=name + "_dw", tag=tags[0], align_bytes=64)
-            ds = keep.tile([P, S], U8, name=name + "_ds", tag=tags[1], align_bytes=64)
-            for dealt, raw in ((dw, words), (ds, scales)):
+        ident = keep.tile([P, P], F32, name="ident")
+        make_identity(nc, ident[:])
+
+        d_wide = tiles("d_wide", 2 * S)
+        gains = d_wide[0][:, S:].rearrange("j (u p e) -> j u p e", u=2, e=2)
+        gain_bank = bank(PACK, [P, PACK, P])
+        for t in range(PACK):
+            nc.tensor.transpose(gain_bank[:, t, :], gain_cols[:, t : t + 1].to_broadcast([P, P]), ident[:])
+        nc.scalar.copy(gains, gain_bank[:].rearrange("j (u e) p -> j u p e", u=2))
+
+        def pick(name, table, offsets, dtype, tag):
+            tile = keep.tile([P, S], dtype, name=name, tag=tag, align_bytes=64)
+            nc.vector.tensor_copy(tile[:], table[:].indirect(offsets[:]))
+            return tile
+
+        def dealt_tiles(name, tags):
+            words = keep.tile([P, 2 * S], U8, name=name + "_dealt_words", tag=tags[0], align_bytes=64)
+            scales = keep.tile([P, S], U8, name=name + "_dealt_scales", tag=tags[1], align_bytes=64)
+            return words, scales
+
+        def deal_runs(name, raw, tags):
+            dealt = dealt_tiles(name, tags)
+            for dst, src in zip(dealt, raw):
                 nc.vector.tensor_copy(
-                    dealt[:].bitcast(I32).rearrange("p (a g w) -> p a g w", a=PACK, g=8),
-                    raw[:].bitcast(I32).rearrange("p (g a w) -> p a g w", a=PACK, g=8),
+                    dst[:].bitcast(I32).rearrange("p (a g w) -> p a g w", a=PACK, g=RUNS),
+                    src[:].bitcast(I32).rearrange("p (g a w) -> p a g w", a=PACK, g=RUNS),
                 )
-            return dw, ds
+            return dealt
 
-        def pick_scales(name, lst, tag):
-            tile = keep.tile([P, S], U8, name=name, tag=tag, align_bytes=64)
-            nc.vector.tensor_copy(tile[:], xs[:].indirect(lst[:]))
-            return tile
+        def deal_fourths(name, raw, tags):
+            dealt = dealt_tiles(name, tags)
+            for dst, src in zip(dealt, raw):
+                nc.vector.tensor_copy(
+                    dst[:].rearrange("p (t m w) -> p t m w", t=PACK, m=P),
+                    src[:].rearrange("p (m t w) -> p t m w", t=PACK, m=P),
+                )
+            return dealt
 
-        def pick_words(name, lst, tag):
-            tile = keep.tile([P, S], U32, name=name, tag=tag, align_bytes=64)
-            nc.vector.tensor_copy(tile[:], xw[:].indirect(lst[:]))
-            return tile
-
-        def product(out, weights, t, codes, scales):
-            dw, ds = weights
+        def product(out, weight, n, codes, scales):
             nc.tensor.matmul_mx(
                 out=out,
-                lhsT=dw[:, 2 * P * t : 2 * P * (t + 1)].bitcast(FP4X4),
-                lhsT_scale=ds[:, P * t : P * (t + 1)],
+                lhsT=weight[0][:, 2 * P * n : 2 * P * (n + 1)].bitcast(FP4X4),
+                lhsT_scale=weight[1][:, P * n : P * (n + 1)],
                 rhs=codes.bitcast(FP8X4),
                 rhs_scale=scales,
                 start=True,
                 stop=True,
             )
 
-        def planes(name):
-            return [keep.tile([P, S], F32, name=f"{name}{t}") for t in range(PACK)]
+        s_two = pick("s_two", xs, l_two, U8, "s_two")
+        s_three = pick("s_three", xs, l_three, U8, "s_three")
+        s_offs = pick("s_offs", xs, l_offs, U8, "s_offs")
+        c_two = pick("c_two", xw, l_two, U32, "c_two")
+        w2 = deal_runs("w2", w2_raw, ("w2_dealt_words", "w2_dealt_scales"))
+        c_offs = pick("c_offs", xw, l_offs, U32, "w2_scales")
+        w1 = deal_runs("w1", w1_raw, ("w2_words", "w1_words"))
+        c_three = pick("c_three", xw, l_three, U32, "w1_scales")
+        w3 = deal_runs("w3", w3_raw, ("xw", "w3_words"))
 
-        def bank(b):
-            return psum.tile([P, S], F32, name=f"bank{b}")
-
-        ident = keep.tile([P, P], F32, name="ident")
-        make_identity(nc, ident[:])
-
-        d_wide = [keep.tile([P, 2 * S], F32, name=f"d_wide{a}") for a in range(PACK)]
-        gains = d_wide[0][:, S:].rearrange("j (u p e) -> j u p e", u=2, e=2)
-        gain_bank = psum.tile([P, PACK, P], F32, name=f"bank{PACK}")
-        for t in range(PACK):
-            nc.tensor.transpose(gain_bank[:, t, :], gain_cols[:, t : t + 1].to_broadcast([P, P]), ident[:])
-        nc.scalar.copy(gains, gain_bank[:].rearrange("j (u e) p -> j u p e", u=2))
-
-        s_two = pick_scales("s_two", l_two, "s_two")
-        s_three = pick_scales("s_three", l_three, "s_three")
-        c_two = pick_words("c_two", l_two, "c_two")
-        w2 = deal_runs("w2", w2w, w2s, ("w2_dw", "w2_ds"))
-        s_offs = pick_scales("s_offs", l_offs, "w2s")
-        c_offs = pick_words("c_offs", l_offs, "w2w")
-        w1 = deal_runs("w1", w1w, w1s, ("xs", "w1w"))
-        c_three = pick_words("c_three", l_three, "c_three")
-        w3 = deal_runs("w3", w3w, w3s, ("xw", "w3w"))
-
-        neg_b, m1 = planes("neg_b"), planes("m1")
-        y_tanh = [keep.tile([P, 2 * S], F32, name=f"y_tanh{a}") for a in range(PACK)]
+        y_tanh, neg_b, m1 = tiles("y_tanh", 2 * S), tiles("neg_b", S), tiles("m1", S)
         for a in range(PACK):
-            d_bank = bank(a)
+            d_bank = bank(a, [P, S])
             product(d_bank[:], w2, a, c_two[:], s_two[:])
             nc.scalar.copy(d_wide[a][:, :S], d_bank[:])
             nc.scalar.activation(y_tanh[a][:, S:], d_bank[:], ACT.Tanh)
-            y_bank = bank(PACK + a)
+            y_bank = bank(PACK + a, [P, S])
             product(y_bank[:], w1, a, c_offs[:], s_offs[:])
             nc.scalar.copy(y_tanh[a][:, :S], y_bank[:])
         for a in range(PACK):
-            b_bank = bank(a)
+            b_bank = bank(a, [P, S])
             product(b_bank[:], w3, a, c_three[:], s_three[:])
             nc.scalar.activation(neg_b[a][:], b_bank[:], ACT.Copy, scale=-1.0)
 
-        n_blocks = S // P
-        z_banks = [bank(PACK + c) for c in range(n_blocks)]
+        z_banks = [bank(PACK + c, [P, S]) for c in range(BLOCKS)]
 
-        def add_turned(c, a, src, start=False, stop=False):
-            nc.tensor.matmul(z_banks[c][:].rearrange("j (g a i) -> j g a i", g=8, a=PACK)[:, :, a, :], src, ident[:], start=start, stop=stop, is_transpose=True)
+        def add_turned(c, a, term, start=False, stop=False):
+            columns = z_banks[c][:].rearrange("j (g a i) -> j g a i", g=RUNS, a=PACK)[:, :, a, :]
+            nc.tensor.matmul(columns, term, ident[:], start=start, stop=stop, is_transpose=True)
 
         gated_last = keep.tile([P, S], F32, name="gated_last")
         gated = [d_wide[a + 1][:, S:] for a in range(PACK - 1)] + [gated_last[:]]
@@ -177,26 +171,27 @@ def tile_picked_triosoftbmaxbhopp_none_po_kernel(
 
         def meet(a):
             nc.vector.tensor_tensor(m1[a][:], y_tanh[a][:].indirect(l_n1[:]), gated[a], ALU.subtract)
-            for c in range(n_blocks):
+            for c in range(BLOCKS):
                 add_turned(c, a, neg_b[a][:, P * c : P * (c + 1)], start=(a == 0))
                 add_turned(c, a, m1[a][:, P * c : P * (c + 1)])
 
         gate(0)
-        w4 = deal("w4", w4w, w4s, ("w3s", "w4w"))
+        w4 = deal_fourths("w4", w4_raw, ("w3_scales", "w4_words"))
         for a in range(1, PACK):
             gate(a)
             meet(a - 1)
 
+        h_window = y_tanh
         h_plain = keep.tile([P, PACK, S], F32, name="h_plain")
-        woven = {}
+        z_woven = {}
 
         def differences(first, count, a):
             lo, hi = P * first, P * (first + count)
-            diff = deep.tile([P, 2, hi - lo], F32, name="diff")
+            diff = ring.tile([P, 2, hi - lo], F32, name="diff")
             nc.vector.tensor_tensor(diff[:, 0, :], neg_b[a][:].indirect(entries(l_n4, lo, hi)), m1[a][:, lo:hi], ALU.add)
             nc.vector.tensor_tensor(diff[:, 1, :], m1[a][:].indirect(entries(l_n3, lo, hi)), neg_b[a][:, lo:hi], ALU.add)
-            excess = deep.tile([P, 2, hi - lo], F32, name="excess")
-            if (first, a) == (n_blocks - 1, PACK - 1):
+            excess = ring.tile([P, 2, hi - lo], F32, name="excess")
+            if (first, a) == (BLOCKS - 1, PACK - 1):
                 for s in range(2):
                     nc.vector.tensor_scalar(excess[:, s, :], diff[:, s, :], 0.0, -1.0, ALU.min, ALU.mult)
             else:
@@ -206,19 +201,19 @@ def tile_picked_triosoftbmaxbhopp_none_po_kernel(
                     add_turned(first + c, a, excess[:, s, P * c : P * (c + 1)], stop=(a == PACK - 1 and s == 1))
 
         def turn_back(c):
-            last = c == n_blocks - 1
-            if c == n_blocks - 2:
-                z_rows = m1[PACK - 1][:, : S // 2].bitcast(BF16).rearrange("j (u p e) -> j u p e", u=2, e=2)
+            last = c == BLOCKS - 1
+            if c == BLOCKS - 2:
+                z_rows = m1[PACK - 1][:, :HALF].bitcast(BF16).rearrange("j (u p e) -> j u p e", u=2, e=2)
             else:
                 z_rows = ring.tile([P, 2, P, 2], BF16, name="z_rows")
-            pairs = psum.tile([P, 2, P], F32, name=f"bank{c % 2}")
+            pairs = bank(c % 2, [P, 2, P])
             sums = z_banks[c][:].rearrange("j (p u e) -> j u p e", u=2, e=2)
             for us in ([slice(0, 1), slice(1, 2)] if last else [slice(0, 2)]):
                 nc.vector.tensor_tensor(z_rows[:, us], sums[:, us], gains[:, us], ALU.mult)
                 for u in range(us.start, us.stop):
                     nc.tensor.transpose(pairs[:, u, :], z_rows[:, u].rearrange("j p e -> j (p e)").bitcast(F32), ident[:])
-            woven[c] = keep.tile([P, S], BF16, name=f"z_woven{c}", align_bytes=64)
-            words = woven[c][:].bitcast(F32).rearrange("p (j u) -> p j u", u=2)
+            z_woven[c] = keep.tile([P, S], BF16, name=f"z_woven{c}", align_bytes=64)
+            words = z_woven[c][:].bitcast(F32).rearrange("p (j u) -> p j u", u=2)
             if last:
                 nc.vector.tensor_copy(words, pairs[:].rearrange("p u j -> p j u"))
             else:
@@ -227,29 +222,29 @@ def tile_picked_triosoftbmaxbhopp_none_po_kernel(
         def second_layer(c):
             codes = keep.tile([P, P], U32, name=f"z_codes{c}", align_bytes=64)
             scales = keep.tile([P, P], U8, name=f"z_scales{c}", align_bytes=64)
-            nc.vector.quantize_mx(out=codes[:].bitcast(FP8X4), scales=scales[:], in_=woven[c][:])
+            nc.vector.quantize_mx(out=codes[:].bitcast(FP8X4), scales=scales[:], in_=z_woven[c][:])
             lo, hi = P * c, P * (c + 1)
-            if c < n_blocks - 1:
-                h_bank = psum.tile([P, PACK, P], F32, name=f"bank{2 + c % 2}")
+            if c < BLOCKS - 1:
+                h_bank = bank(2 + c % 2, [P, PACK, P])
                 for t in range(PACK):
                     product(h_bank[:, t, :], w4, t, codes[:], scales[:])
-                nc.scalar.activation(y_tanh[0][:, lo:hi], h_bank[:, 0, :], ACT.Copy, scale=2.0)
+                nc.scalar.activation(h_window[0][:, lo:hi], h_bank[:, 0, :], ACT.Copy, scale=2.0)
                 nc.scalar.activation(h_plain[:, :, lo:hi], h_bank[:], ACT.Copy, scale=2.0)
                 for t in range(1, PACK):
-                    nc.scalar.activation(y_tanh[t][:, lo:hi], h_bank[:, t, :], ACT.Copy, scale=2.0)
+                    nc.scalar.activation(h_window[t][:, lo:hi], h_bank[:, t, :], ACT.Copy, scale=2.0)
             else:
-                h_last = [psum.tile([P, P], F32, name=f"bank{PACK + t}") for t in range(PACK)]
+                h_last = [bank(PACK + t, [P, P]) for t in range(PACK)]
                 for t in range(PACK):
                     product(h_last[t][:], w4, t, codes[:], scales[:])
-                nc.vector.tensor_scalar(y_tanh[0][:, lo:hi], h_last[0][:], 2.0, None, ALU.mult)
+                nc.vector.tensor_scalar(h_window[0][:, lo:hi], h_last[0][:], 2.0, None, ALU.mult)
                 nc.vector.tensor_scalar(h_plain[:, 0, lo:hi], h_last[0][:], 2.0, None, ALU.mult)
                 for t in range(1, PACK):
-                    nc.scalar.activation(y_tanh[t][:, lo:hi], h_last[t][:], ACT.Copy, scale=2.0)
+                    nc.scalar.activation(h_window[t][:, lo:hi], h_last[t][:], ACT.Copy, scale=2.0)
                     nc.scalar.activation(h_plain[:, t, lo:hi], h_last[t][:], ACT.Copy, scale=2.0)
 
-        for a in range(PACK):
-            if a == 1:
-                meet(PACK - 1)
+        differences(0, 2, 0)
+        meet(PACK - 1)
+        for a in range(1, PACK):
             differences(0, 2, a)
         for a in range(PACK):
             differences(2, 1, a)
@@ -259,48 +254,51 @@ def tile_picked_triosoftbmaxbhopp_none_po_kernel(
             differences(3, 1, a)
             if a in (0, 1):
                 second_layer(a)
-        turn_back(n_blocks - 2)
-        turn_back(n_blocks - 1)
-        second_layer(n_blocks - 2)
-        second_layer(n_blocks - 1)
+        turn_back(2)
+        turn_back(3)
+        second_layer(2)
+        second_layer(3)
 
-        st2, sig = planes("st2"), planes("sig")
-        half = S // 2
-        res = keep.tile([P, 2, PACK, half], F32, name="res")
-        rows = out_0.rearrange("(p t) (c j) -> p c t j", t=PACK, c=2)
+        st2, sig = tiles("st2", S), tiles("sig", S)
+        res = keep.tile([P, 2, PACK, HALF], F32, name="res")
+        out_rows = out_0.rearrange("(p t) (v j) -> p v t j", t=PACK, v=2)
 
-        def finish(t, cs):
-            cols = slice(half * cs.start, half * cs.stop)
+        def finish(t, halves):
+            cols = slice(HALF * halves.start, HALF * halves.stop)
             nc.vector.scalar_tensor_tensor(
-                res[:, cs, t, :],
-                sig[t][:, cols].rearrange("p (c j) -> p c j", j=half),
+                res[:, halves, t, :],
+                sig[t][:, cols].rearrange("p (v j) -> p v j", j=HALF),
                 -0.5,
-                st2[t][:, cols].rearrange("p (c j) -> p c j", j=half),
+                st2[t][:, cols].rearrange("p (v j) -> p v j", j=HALF),
                 ALU.add,
                 ALU.mult,
             )
-            nc.sync.dma_start(rows[:, cs, t, :], res[:, cs, t, :])
+            nc.sync.dma_start(out_rows[:, halves, t, :], res[:, halves, t, :])
 
         for t in range(PACK):
-            nc.vector.tensor_tensor(st2[t][:], y_tanh[t][:].indirect(l_n5[:]), h_plain[:, t, :], ALU.add)
-            for lo, hi in HALVES:
-                nc.scalar.activation(sig[t][:, lo:hi], st2[t][:].indirect(entries(l_n6, lo, hi)), ACT.Sigmoid)
+            nc.vector.tensor_tensor(st2[t][:], h_window[t][:].indirect(l_n5[:]), h_plain[:, t, :], ALU.add)
+            for lo in (0, HALF):
+                nc.scalar.activation(sig[t][:, lo : lo + HALF], st2[t][:].indirect(entries(l_n6, lo, lo + HALF)), ACT.Sigmoid)
             if t == PACK - 2:
                 finish(0, slice(0, 2))
                 finish(1, slice(0, 2))
-        finish(2, slice(0, 2))
-        finish(3, slice(0, 1))
-        finish(3, slice(1, 2))
+
+        o_woven = [keep.tile([P, HALF, PACK], BF16, name=f"o_woven{v}", align_bytes=64) for v in range(2)]
         o_codes = keep.tile([P, S], U32, name="o_codes", align_bytes=64)
         o_scales = keep.tile([P, S], U8, name="o_scales", align_bytes=64)
-        woven_out = [keep.tile([P, hi - lo, PACK], BF16, name=f"o_woven{c}", align_bytes=64) for c, (lo, hi) in enumerate(HALVES)]
-        nc.scalar.copy(woven_out[0][:], res[:, 0].rearrange("p t j -> p j t"))
-        nc.vector.tensor_copy(woven_out[1][:], res[:, 1].rearrange("p t j -> p j t"))
+        finish(2, slice(0, 2))
+        finish(3, slice(0, 1))
+        nc.scalar.copy(o_woven[0][:, :SCALAR_WEAVE, :], res[:, 0, :, :SCALAR_WEAVE].rearrange("p t j -> p j t"))
+        nc.vector.tensor_copy(o_woven[0][:, SCALAR_WEAVE:, :], res[:, 0, :, SCALAR_WEAVE:].rearrange("p t j -> p j t"))
+        finish(3, slice(1, 2))
+        nc.vector.tensor_copy(o_woven[1][:], res[:, 1].rearrange("p t j -> p j t"))
         words_out = out_1[0].rearrange("p c r -> p (c r)").bitcast(I32)
-        for c in (1, 0):
-            lo, hi = HALVES[c]
-            nc.vector.quantize_mx(out=o_codes[:, lo:hi].bitcast(FP8X4), scales=o_scales[:, lo:hi], in_=woven_out[c][:].rearrange("p j t -> p (j t)"))
-            nc.sync.dma_start(words_out[:, lo:hi], o_codes[:, lo:hi].bitcast(I32))
+        for v in range(2):
+            cols = slice(HALF * v, HALF * (v + 1))
+            nc.vector.quantize_mx(
+                out=o_codes[:, cols].bitcast(FP8X4), scales=o_scales[:, cols], in_=o_woven[v][:].rearrange("p j t -> p (j t)")
+            )
+            nc.sync.dma_start(words_out[:, cols], o_codes[:, cols].bitcast(I32))
         for q in range(4):
             queue = nc.scalar if q % 2 else nc.sync
             queue.dma_start(out_2[0][4 * q : 4 * q + 4, :].bitcast(I32), o_scales[32 * q : 32 * q + 4, :].bitcast(I32))

from contextlib import ExitStack

import concourse.mybir as mybir
from concourse.masks import make_identity

F32 = mybir.dt.float32
BF16 = mybir.dt.bfloat16
I32 = mybir.dt.int32
U32 = mybir.dt.uint32
U16 = mybir.dt.uint16
U8 = mybir.dt.uint8
FP8X4 = mybir.dt.float8_e4m3fn_x4
FP4X4 = mybir.dt.float4_e2m1fn_x4
ALU = mybir.AluOpType
ACT = mybir.ActivationFunctionType

P = 128
PACK = 4
RUNS = 8
T = 2048
S = 512
BLOCKS = S // P
HALF = S // 2
SCALAR_WEAVE = 192
FLOPS = 4 * 2 * 512 * 512 * 512


def tile_picked_triosoftbmaxbhopp_none_po_kernel(
    tc, x_words, x_scales, w1_words, w1_scales, w2_words, w2_scales, w3_words, w3_scales, gn, w4_words, w4_scales,
    offs, two, three, n1, n2, n3, n4, n5, n6, out_0, out_1, out_2,
):
    nc = tc.nc
    with ExitStack() as ctx:
        keep = ctx.enter_context(tc.tile_pool(name="keep", bufs=1))
        ring = ctx.enter_context(tc.tile_pool(name="ring", bufs=3))
        psum = ctx.enter_context(tc.psum_pool(name="psum", bufs=1))

        def bank(b, shape):
            return psum.tile(shape, F32, name=f"bank{b}")

        def tiles(name, width):
            return [keep.tile([P, width], F32, name=f"{name}{n}") for n in range(PACK)]

        def entries(offsets, lo, hi):
            return offsets[:, lo // 16 : hi // 16]

        def load_list(name, src):
            tile = keep.tile([P, S // 16], U16, name=name)
            nc.sync.dma_start(tile[:], src)
            return tile

        def load_scales(name, src, width, queues):
            tile = keep.tile([P, width], U8, name=name, tag=name, align_bytes=64)
            for q in range(4):
                rows = src[0][4 * q : 4 * q + 4, :].bitcast(I32).unsqueeze(0).to_broadcast([8, 4, width // 4])
                queues[q % len(queues)].dma_start(tile[32 * q : 32 * q + 32, :].bitcast(I32), rows)
            return tile

        def load_weight(name, words, scales):
            tile = keep.tile([P, 2 * S], U8, name=name + "_words", tag=name + "_words", align_bytes=64)
            nc.sync.dma_start(tile[:].bitcast(I32), words[0].bitcast(I32))
            return tile, load_scales(name + "_scales", scales, S, [nc.sync])

        l_two = load_list("l_two", two)
        xs = load_scales("xs", x_scales, T, [nc.sync, nc.scalar])
        l_three = load_list("l_three", three)
        l_offs = load_list("l_offs", offs)
        xw = keep.tile([P, T], U32, name="xw", tag="xw", align_bytes=64)
        nc.sync.dma_start(xw[:].bitcast(I32), x_words[0].rearrange("p c r -> p (c r)").bitcast(I32))
        w2_raw = load_weight("w2", w2_words, w2_scales)
        gain_cols = keep.tile([P, PACK], F32, name="gain_cols")
        nc.sync.dma_start(gain_cols[:], gn.rearrange("(p t) o -> p (t o)", t=PACK))
        w1_raw = load_weight("w1", w1_words, w1_scales)
        l_n2 = load_list("l_n2", n2)
        w3_raw = load_weight("w3", w3_words, w3_scales)
        l_n1 = load_list("l_n1", n1)
        w4_raw = load_weight("w4", w4_words, w4_scales)
        l_n4 = load_list("l_n4", n4)
        l_n3 = load_list("l_n3", n3)
        l_n5 = load_list("l_n5", n5)
        l_n6 = load_list("l_n6", n6)

        warm = keep.tile([P, 2], F32, name="warm")
        nc.gpsimd.memset(warm[:], 0.0)
        nc.scalar.activation(warm[:, 1:2], warm[:, 0:1], ACT.Sigmoid)

        ident = keep.tile([P, P], F32, name="ident")
        make_identity(nc, ident[:])

        d_wide = tiles("d_wide", 2 * S)
        gains = d_wide[0][:, S:].rearrange("j (u p e) -> j u p e", u=2, e=2)
        gain_bank = bank(PACK, [P, PACK, P])
        for t in range(PACK):
            nc.tensor.transpose(gain_bank[:, t, :], gain_cols[:, t : t + 1].to_broadcast([P, P]), ident[:])
        nc.scalar.copy(gains, gain_bank[:].rearrange("j (u e) p -> j u p e", u=2))

        def pick(name, table, offsets, dtype, tag):
            tile = keep.tile([P, S], dtype, name=name, tag=tag, align_bytes=64)
            nc.vector.tensor_copy(tile[:], table[:].indirect(offsets[:]))
            return tile

        def dealt_tiles(name, tags):
            words = keep.tile([P, 2 * S], U8, name=name + "_dealt_words", tag=tags[0], align_bytes=64)
            scales = keep.tile([P, S], U8, name=name + "_dealt_scales", tag=tags[1], align_bytes=64)
            return words, scales

        def deal_runs(name, raw, tags):
            dealt = dealt_tiles(name, tags)
            for dst, src in zip(dealt, raw):
                nc.vector.tensor_copy(
                    dst[:].bitcast(I32).rearrange("p (a g w) -> p a g w", a=PACK, g=RUNS),
                    src[:].bitcast(I32).rearrange("p (g a w) -> p a g w", a=PACK, g=RUNS),
                )
            return dealt

        def deal_fourths(name, raw, tags):
            dealt = dealt_tiles(name, tags)
            for dst, src in zip(dealt, raw):
                nc.vector.tensor_copy(
                    dst[:].rearrange("p (t m w) -> p t m w", t=PACK, m=P),
                    src[:].rearrange("p (m t w) -> p t m w", t=PACK, m=P),
                )
            return dealt

        def product(out, weight, n, codes, scales):
            nc.tensor.matmul_mx(
                out=out,
                lhsT=weight[0][:, 2 * P * n : 2 * P * (n + 1)].bitcast(FP4X4),
                lhsT_scale=weight[1][:, P * n : P * (n + 1)],
                rhs=codes.bitcast(FP8X4),
                rhs_scale=scales,
                start=True,
                stop=True,
            )

        s_two = pick("s_two", xs, l_two, U8, "s_two")
        s_three = pick("s_three", xs, l_three, U8, "s_three")
        s_offs = pick("s_offs", xs, l_offs, U8, "s_offs")
        c_two = pick("c_two", xw, l_two, U32, "c_two")
        w2 = deal_runs("w2", w2_raw, ("w2_dealt_words", "w2_dealt_scales"))
        c_offs = pick("c_offs", xw, l_offs, U32, "w2_scales")
        w1 = deal_runs("w1", w1_raw, ("w2_words", "w1_words"))
        c_three = pick("c_three", xw, l_three, U32, "w1_scales")
        w3 = deal_runs("w3", w3_raw, ("xw", "w3_words"))

        y_tanh, neg_b, m1 = tiles("y_tanh", 2 * S), tiles("neg_b", S), tiles("m1", S)
        for a in range(PACK):
            d_bank = bank(a, [P, S])
            product(d_bank[:], w2, a, c_two[:], s_two[:])
            nc.scalar.copy(d_wide[a][:, :S], d_bank[:])
            nc.scalar.activation(y_tanh[a][:, S:], d_bank[:], ACT.Tanh)
            y_bank = bank(PACK + a, [P, S])
            product(y_bank[:], w1, a, c_offs[:], s_offs[:])
            nc.scalar.copy(y_tanh[a][:, :S], y_bank[:])
        for a in range(PACK):
            b_bank = bank(a, [P, S])
            product(b_bank[:], w3, a, c_three[:], s_three[:])
            nc.scalar.activation(neg_b[a][:], b_bank[:], ACT.Copy, scale=-1.0)

        z_banks = [bank(PACK + c, [P, S]) for c in range(BLOCKS)]

        def add_turned(c, a, term, start=False, stop=False):
            columns = z_banks[c][:].rearrange("j (g a i) -> j g a i", g=RUNS, a=PACK)[:, :, a, :]
            nc.tensor.matmul(columns, term, ident[:], start=start, stop=stop, is_transpose=True)

        gated_last = keep.tile([P, S], F32, name="gated_last")
        gated = [d_wide[a + 1][:, S:] for a in range(PACK - 1)] + [gated_last[:]]

        def gate(a):
            nc.vector.tensor_tensor(gated[a], d_wide[a][:].indirect(l_n2[:]), y_tanh[a][:, S:], ALU.mult)

        def meet(a):
            nc.vector.tensor_tensor(m1[a][:], y_tanh[a][:].indirect(l_n1[:]), gated[a], ALU.subtract)
            for c in range(BLOCKS):
                add_turned(c, a, neg_b[a][:, P * c : P * (c + 1)], start=(a == 0))
                add_turned(c, a, m1[a][:, P * c : P * (c + 1)])

        gate(0)
        w4 = deal_fourths("w4", w4_raw, ("w3_scales", "w4_words"))
        for a in range(1, PACK):
            gate(a)
            meet(a - 1)

        h_window = y_tanh
        h_plain = keep.tile([P, PACK, S], F32, name="h_plain")
        z_woven = {}

        def differences(first, count, a):
            lo, hi = P * first, P * (first + count)
            diff = ring.tile([P, 2, hi - lo], F32, name="diff")
            nc.vector.tensor_tensor(diff[:, 0, :], neg_b[a][:].indirect(entries(l_n4, lo, hi)), m1[a][:, lo:hi], ALU.add)
            nc.vector.tensor_tensor(diff[:, 1, :], m1[a][:].indirect(entries(l_n3, lo, hi)), neg_b[a][:, lo:hi], ALU.add)
            excess = ring.tile([P, 2, hi - lo], F32, name="excess")
            if (first, a) == (BLOCKS - 1, PACK - 1):
                for s in range(2):
                    nc.vector.tensor_scalar(excess[:, s, :], diff[:, s, :], 0.0, -1.0, ALU.min, ALU.mult)
            else:
                nc.scalar.activation(excess[:], diff[:], ACT.Relu, scale=-1.0)
            for c in range(count):
                for s in range(2):
                    add_turned(first + c, a, excess[:, s, P * c : P * (c + 1)], stop=(a == PACK - 1 and s == 1))

        def turn_back(c):
            last = c == BLOCKS - 1
            if c == BLOCKS - 2:
                z_rows = m1[PACK - 1][:, :HALF].bitcast(BF16).rearrange("j (u p e) -> j u p e", u=2, e=2)
            else:
                z_rows = ring.tile([P, 2, P, 2], BF16, name="z_rows")
            pairs = bank(c % 2, [P, 2, P])
            sums = z_banks[c][:].rearrange("j (p u e) -> j u p e", u=2, e=2)
            for us in ([slice(0, 1), slice(1, 2)] if last else [slice(0, 2)]):
                nc.vector.tensor_tensor(z_rows[:, us], sums[:, us], gains[:, us], ALU.mult)
                for u in range(us.start, us.stop):
                    nc.tensor.transpose(pairs[:, u, :], z_rows[:, u].rearrange("j p e -> j (p e)").bitcast(F32), ident[:])
            z_woven[c] = keep.tile([P, S], BF16, name=f"z_woven{c}", align_bytes=64)
            words = z_woven[c][:].bitcast(F32).rearrange("p (j u) -> p j u", u=2)
            if last:
                nc.vector.tensor_copy(words, pairs[:].rearrange("p u j -> p j u"))
            else:
                nc.scalar.copy(words, pairs[:].rearrange("p u j -> p j u"))

        def second_layer(c):
            codes = keep.tile([P, P], U32, name=f"z_codes{c}", align_bytes=64)
            scales = keep.tile([P, P], U8, name=f"z_scales{c}", align_bytes=64)
            nc.vector.quantize_mx(out=codes[:].bitcast(FP8X4), scales=scales[:], in_=z_woven[c][:])
            lo, hi = P * c, P * (c + 1)
            if c < BLOCKS - 1:
                h_bank = bank(2 + c % 2, [P, PACK, P])
                for t in range(PACK):
                    product(h_bank[:, t, :], w4, t, codes[:], scales[:])
                nc.scalar.activation(h_window[0][:, lo:hi], h_bank[:, 0, :], ACT.Copy, scale=2.0)
                nc.scalar.activation(h_plain[:, :, lo:hi], h_bank[:], ACT.Copy, scale=2.0)
                for t in range(1, PACK):
                    nc.scalar.activation(h_window[t][:, lo:hi], h_bank[:, t, :], ACT.Copy, scale=2.0)
            else:
                h_last = [bank(PACK + t, [P, P]) for t in range(PACK)]
                for t in range(PACK):
                    product(h_last[t][:], w4, t, codes[:], scales[:])
                nc.vector.tensor_scalar(h_window[0][:, lo:hi], h_last[0][:], 2.0, None, ALU.mult)
                nc.vector.tensor_scalar(h_plain[:, 0, lo:hi], h_last[0][:], 2.0, None, ALU.mult)
                for t in range(1, PACK):
                    nc.scalar.activation(h_window[t][:, lo:hi], h_last[t][:], ACT.Copy, scale=2.0)
                    nc.scalar.activation(h_plain[:, t, lo:hi], h_last[t][:], ACT.Copy, scale=2.0)

        differences(0, 2, 0)
        meet(PACK - 1)
        for a in range(1, PACK):
            differences(0, 2, a)
        for a in range(PACK):
            differences(2, 1, a)
            if a in (1, 2):
                turn_back(a - 1)
        for a in range(PACK):
            differences(3, 1, a)
            if a in (0, 1):
                second_layer(a)
        turn_back(2)
        turn_back(3)
        second_layer(2)
        second_layer(3)

        st2, sig = tiles("st2", S), tiles("sig", S)
        res = keep.tile([P, 2, PACK, HALF], F32, name="res")
        out_rows = out_0.rearrange("(p t) (v j) -> p v t j", t=PACK, v=2)

        def finish(t, halves):
            cols = slice(HALF * halves.start, HALF * halves.stop)
            nc.vector.scalar_tensor_tensor(
                res[:, halves, t, :],
                sig[t][:, cols].rearrange("p (v j) -> p v j", j=HALF),
                -0.5,
                st2[t][:, cols].rearrange("p (v j) -> p v j", j=HALF),
                ALU.add,
                ALU.mult,
            )
            nc.sync.dma_start(out_rows[:, halves, t, :], res[:, halves, t, :])

        for t in range(PACK):
            nc.vector.tensor_tensor(st2[t][:], h_window[t][:].indirect(l_n5[:]), h_plain[:, t, :], ALU.add)
            for lo in (0, HALF):
                nc.scalar.activation(sig[t][:, lo : lo + HALF], st2[t][:].indirect(entries(l_n6, lo, lo + HALF)), ACT.Sigmoid)
            if t == PACK - 2:
                finish(0, slice(0, 2))
                finish(1, slice(0, 2))

        o_woven = [keep.tile([P, HALF, PACK], BF16, name=f"o_woven{v}", align_bytes=64) for v in range(2)]
        o_codes = keep.tile([P, S], U32, name="o_codes", align_bytes=64)
        o_scales = keep.tile([P, S], U8, name="o_scales", align_bytes=64)
        finish(2, slice(0, 2))
        finish(3, slice(0, 1))
        nc.scalar.copy(o_woven[0][:, :SCALAR_WEAVE, :], res[:, 0, :, :SCALAR_WEAVE].rearrange("p t j -> p j t"))
        nc.vector.tensor_copy(o_woven[0][:, SCALAR_WEAVE:, :], res[:, 0, :, SCALAR_WEAVE:].rearrange("p t j -> p j t"))
        finish(3, slice(1, 2))
        nc.vector.tensor_copy(o_woven[1][:], res[:, 1].rearrange("p t j -> p j t"))
        words_out = out_1[0].rearrange("p c r -> p (c r)").bitcast(I32)
        for v in range(2):
            cols = slice(HALF * v, HALF * (v + 1))
            nc.vector.quantize_mx(
                out=o_codes[:, cols].bitcast(FP8X4), scales=o_scales[:, cols], in_=o_woven[v][:].rearrange("p j t -> p (j t)")
            )
            nc.sync.dma_start(words_out[:, cols], o_codes[:, cols].bitcast(I32))
        for q in range(4):
            queue = nc.scalar if q % 2 else nc.sync
            queue.dma_start(out_2[0][4 * q : 4 * q + 4, :].bitcast(I32), o_scales[32 * q : 32 * q + 4, :].bitcast(I32))
